import numpy as np
import ml_dtypes


def mxq(x, axis, fmt="e4m3"):
    dtype, down = {"e4m3": (ml_dtypes.float8_e4m3fn, 7), "e5m2": (ml_dtypes.float8_e5m2, 14)}[fmt]
    v = np.moveaxis(np.asarray(x, np.float32).astype(ml_dtypes.bfloat16).astype(np.float64), axis, -1)
    blocks = v.reshape(v.shape[:-1] + (-1, 32))
    amax = np.abs(blocks).max(-1, keepdims=True)
    byte = np.maximum(np.where(amax > 0, np.frexp(amax)[1] - 1 + 127, 0) - down, 1)
    scale = np.exp2(byte - 127.0)
    codes = (blocks / scale).astype(np.float32).astype(dtype).astype(np.float64)
    return np.moveaxis((codes * scale).reshape(v.shape), -1, axis)


WIDE = False


def mx_kscale(k):
    if not WIDE:
        return np.ones(k)
    levels = np.array([10, -10, 5, -5, 0])
    if k % 512:
        return np.exp2(np.random.permutation(np.resize(levels, k // 32))).repeat(32)
    a = np.empty((k // 512, 16))
    for p in range(k // 512):
        a[p, :8] = np.random.permutation(np.resize(levels, 8))
        for g in range(8):
            far = levels[np.abs(levels - a[p, g]) >= 10]
            a[p, g + 8] = far[np.random.randint(len(far))]
    return np.exp2(a.ravel()).repeat(32)


def f64(x):
    return np.asarray(x).astype(np.float64)


def striped(idx):
    return np.tile(idx.reshape(-1, 16).T, (8, 1)).astype(np.uint16)


def unstriped(offs):
    return offs[:16].T.reshape(-1).astype(np.int64)


E2M1 = np.array([0.0, 0.5, 1.0, 1.5, 2.0, 3.0, 4.0, 6.0, -0.0, -0.5, -1.0, -1.5, -2.0, -3.0, -4.0, -6.0])


def pack_weight(w, fmt):
    k, n = w.shape
    w = f64(np.asarray(w, np.float32).astype(ml_dtypes.bfloat16)).reshape(k // 32, 32, n)
    amax = np.abs(w).max(1)
    if fmt == "e4m3":
        byte = np.frexp(amax)[1] - 1 + 127 - 7
    else:
        mant, ex = np.frexp(amax / 6.0)
        byte = np.where(mant > 0.5, ex, ex - 1) + 127
    byte = np.clip(np.where(amax > 0, byte, 1), 1, 254)
    scaled = (w * np.exp2(127.0 - byte)[:, None, :]).reshape(k, n).astype(np.float32)
    by_word = np.ascontiguousarray(scaled.reshape(k // 512, 128, 4, n).transpose(0, 1, 3, 2))
    if fmt == "e4m3":
        words = by_word.astype(ml_dtypes.float8_e4m3fn).view(np.uint8)
    else:
        c = by_word.astype(ml_dtypes.float4_e2m1fn).view(np.uint8) & 0xF
        words = (c[..., 0::2] | (c[..., 1::2] << 4)).reshape(k // 512, 128, 2 * n)
    return np.ascontiguousarray(words), np.ascontiguousarray(byte.astype(np.uint8).reshape(k // 512, 16, n))


def unpack_weight(words, scales, fmt):
    g, _, n = scales.shape
    words = np.ascontiguousarray(words).reshape(g, 128, n, -1)
    if fmt == "e4m3":
        vals = words.view(ml_dtypes.float8_e4m3fn).astype(np.float64)
    else:
        nib = np.empty((g, 128, n, 4), np.uint8)
        nib[..., 0::2] = words & 0xF
        nib[..., 1::2] = words >> 4
        vals = E2M1[nib]
    vals = vals * np.repeat(np.exp2(scales.astype(np.float64) - 127.0), 8, axis=1)[..., None]
    return vals.transpose(0, 1, 3, 2).reshape(g * 512, n)


def gelu(v):
    return 0.5 * v * (1.0 + np.tanh(np.sqrt(2.0 / np.pi) * (v + 0.044715 * v**3)))


K, T, E, C, H, HS, N = 512, 768, 6, 256, 512, 512, 256


def by_expert(wq, xq):
    return np.concatenate([wq[e].T @ xq[:, e * C:(e + 1) * C] for e in range(E)], axis=1)


def setup_inputs():
    n = np.random.standard_normal
    s = mx_kscale(K)
    u = mx_kscale(H)
    v = mx_kscale(HS)
    first = np.random.permutation(np.repeat(np.arange(E), T // E))
    second = (first + 1 + np.random.permutation(np.repeat(np.arange(E - 1), -(-T // (E - 1)))[:T])) % E
    while np.bincount(second, minlength=E).max() != T // E:
        load = np.bincount(second, minlength=E); hi, lo = int(load.argmax()), int(load.argmin())
        t = np.flatnonzero((second == hi) & (first != lo))[0]; second[t] = lo
    slot_token = np.empty(E * C, np.int64); pos = np.empty((2, T), np.int64); fill = np.zeros(E, np.int64)
    place = np.stack([np.random.permutation(C) for _ in range(E)])
    for r, deal in enumerate((first, second)):
        for t in np.random.permutation(T):
            e = deal[t]; j = e * C + place[e, fill[e]]; fill[e] += 1; slot_token[j] = t; pos[r, t] = j
    g = np.random.uniform(0.2, 0.8, T)
    x = pack_weight(n((K, T)) * s[:, None], "e4m3")
    w1 = [pack_weight(m, "e2m1") for m in n((E, K, H)) / np.sqrt(K) / s[None, :, None]]
    w3 = [pack_weight(m, "e2m1") for m in n((E, K, H)) / np.sqrt(K) / s[None, :, None] * u]
    w2 = [pack_weight(m, "e2m1") for m in n((E, H, N)) / np.sqrt(H) / u[None, :, None]]
    w1s = pack_weight(n((K, HS)) / np.sqrt(K) / s[:, None], "e4m3")
    w3s = pack_weight(n((K, HS)) / np.sqrt(K) / s[:, None] * v, "e4m3")
    w2s = pack_weight(n((HS, N)) / np.sqrt(HS) / v[:, None], "e4m3")
    return {
        "x_words": x[0],
        "x_scales": x[1],
        "w1_words": np.stack([m[0] for m in w1]),
        "w1_scales": np.stack([m[1] for m in w1]),
        "w3_words": np.stack([m[0] for m in w3]),
        "w3_scales": np.stack([m[1] for m in w3]),
        "w2_words": np.stack([m[0] for m in w2]),
        "w2_scales": np.stack([m[1] for m in w2]),
        "w1s_words": w1s[0],
        "w1s_scales": w1s[1],
        "w3s_words": w3s[0],
        "w3s_scales": w3s[1],
        "w2s_words": w2s[0],
        "w2s_scales": w2s[1],
        "gate": np.stack([np.tile(g, (128, 1)), np.tile(1.0 - g, (128, 1))]).astype(np.float32),
        "offs": striped(slot_token),
        "pos1": striped(pos[0]),
        "pos2": striped(pos[1]),
    }


def reference(x_words, x_scales, w1_words, w1_scales, w3_words, w3_scales, w2_words, w2_scales, w1s_words, w1s_scales, w3s_words, w3s_scales, w2s_words, w2s_scales, gate, offs, pos1, pos2):
    w1 = np.stack([unpack_weight(w1_words[e], w1_scales[e], "e2m1") for e in range(E)])
    w3 = np.stack([unpack_weight(w3_words[e], w3_scales[e], "e2m1") for e in range(E)])
    w2 = np.stack([unpack_weight(w2_words[e], w2_scales[e], "e2m1") for e in range(E)])
    w1s = unpack_weight(w1s_words, w1s_scales, "e4m3")
    w3s = unpack_weight(w3s_words, w3s_scales, "e4m3")
    w2s = unpack_weight(w2s_words, w2s_scales, "e4m3")
    idx = unstriped(offs)
    x = unpack_weight(x_words, x_scales, "e4m3")
    hs = gelu(w1s.T @ x) * (w3s.T @ x)
    ys = w2s.T @ mxq(hs, 0, "e4m3")
    h = gelu(by_expert(w1, x[:, idx])) * by_expert(w3, x[:, idx])
    y = by_expert(w2, mxq(h, 0, "e4m3"))
    c = sum(f64(gate[r, :1]) * y[:, unstriped(p)] for r, p in enumerate((pos1, pos2)))
    return ys + c

@@ -1,0 +1,206 @@
+from contextlib import ExitStack
+
+import concourse.mybir as mybir
+from concourse.masks import make_identity
+
+K, T, E, C, H, N = 512, 768, 6, 256, 512, 256
+S = E * C
+FLOPS = 2 * (S + T) * (2 * K * H + H * N)
+
+F32 = mybir.dt.float32
+BF16 = mybir.dt.bfloat16
+I32 = mybir.dt.int32
+U32 = mybir.dt.uint32
+U16 = mybir.dt.uint16
+U8 = mybir.dt.uint8
+FP8X4 = mybir.dt.float8_e4m3fn_x4
+FP4X4 = mybir.dt.float4_e2m1fn_x4
+GELU = mybir.ActivationFunctionType.Gelu_apprx_tanh
+MULT = mybir.AluOpType.mult
+ADD = mybir.AluOpType.add
+
+P = 128
+G = 256
+HELD_WORDS = 4
+HELD_SCALES = 2
+ORDER = [0, 1, 2, 3, 4, 5, 6, 7, 8]
+STEPS = [["words",2,0,"a"],["words",0,0,"a"],["words",3,0,"a"],["words",1,0,"a"],["scales",1,0,"a"],["scales",0,0,"a"],["first",0,[6,1,4,3],"a"],["scales",2,0,"a"],["first",1,[2,5,6,0],"a"],["scales",3,0,"a"],["first",2,[3,6,0,5],"a"],["turn",1,7,"a"],["scales",4,0,"a"],["turn",0,4,"a"],["words",4,0,"a"],["first",3,[2,3,4,7],"a"],["scales",5,0,"a"],["second",1,1,"a"],["turn",2,5,"a"],["words",5,0,"a"],["second",2,3,"v"],["first",4,[2,0,4,5],"a"],["second",0,6,"a"],["turn",3,6,"a"],["first",5,[1,2,6,7],"a"],["turn",4,5,"v"],["first",6,[0,1,4,5],"a"],["turn",5,6,"v"],["second",3,3,"a"],["first",7,[2,0,6,7],"a"],["first",8,[1,7,3,5],"a"],["second",4,4,"a"],["turn",7,1,"a"],["turn",6,3,"a"],["turn",8,1,"a"],["second",8,0,"a"],["second",6,0,"a"],["second",7,0,"a"],["second",5,2,"a"]]
+
+
+def load_scales(queue, quadrants, *pairs):
+    for q in quadrants:
+        for plane, scales in pairs:
+            queue.dma_start(
+                out=plane[32 * q : 32 * q + 4, :, :].bitcast(I32),
+                in_=scales[:, 4 * q : 4 * q + 4, :].rearrange("m r w -> r m w").bitcast(I32),
+            )
+
+
+def tile_moe_shf_glu_gelu_kernel(
+    tc, x_words, x_scales, w1_words, w1_scales, w3_words, w3_scales, w2_words, w2_scales,
+    w1s_words, w1s_scales, w3s_words, w3s_scales, w2s_words, w2s_scales, gate, offs, pos1, pos2, out,
+):
+    nc = tc.nc
+    with ExitStack() as ctx:
+        keep = ctx.enter_context(tc.tile_pool(name="keep", bufs=1))
+        psum = ctx.enter_context(tc.psum_pool(name="psum", bufs=1))
+
+        def ring(name, count, shape, dtype):
+            return [keep.tile(shape, dtype, name="%s%d" % (name, k), align_bytes=64) for k in range(count)]
+
+        offs_t = keep.tile([P, S // 16], U16, name="offs_t")
+        pos1_t = keep.tile([P, T // 16], U16, name="pos1_t")
+        pos2_t = keep.tile([P, T // 16], U16, name="pos2_t")
+        xw = keep.tile([P, T], I32, name="xw", align_bytes=64)
+        xs = keep.tile([P, 1, T], U8, name="xs", align_bytes=64)
+        s1 = keep.tile([P, E, H], U8, name="s1", align_bytes=64)
+        s3 = keep.tile([P, E, H], U8, name="s3", align_bytes=64)
+        s2 = keep.tile([P, E, N], U8, name="s2", align_bytes=64)
+        s1s = keep.tile([P, 1, H], U8, name="s1s", align_bytes=64)
+        s3s = keep.tile([P, 1, H], U8, name="s3s", align_bytes=64)
+        s2s = keep.tile([P, 1, N], U8, name="s2s", align_bytes=64)
+        w1s = keep.tile([P, H], I32, name="w1s", align_bytes=64)
+        w3s = keep.tile([P, H], I32, name="w3s", align_bytes=64)
+        w2s = keep.tile([P, N], I32, name="w2s", align_bytes=64)
+        gate_t = keep.tile([P, 2, T], F32, name="gate_t")
+        ident = keep.tile([P, P], F32, name="ident")
+
+        for plane in (xs,):
+            nc.gpsimd.memset(plane[:].bitcast(I32), 0)
+        for plane in (s1, s3, s2, s1s, s3s, s2s):
+            nc.vector.memset(plane[:].bitcast(I32), 0)
+        make_identity(nc, ident[:])
+
+        w1, w3, w2 = {}, {}, {}
+
+        def load_fp4(words, held, name, lo, hi):
+            t = keep.tile([P, hi - lo, words.shape[3]], U8, name="%s_%d" % (name, lo), align_bytes=64)
+            nc.sync.dma_start(out=t[:].bitcast(I32), in_=words[lo:hi, 0].rearrange("e p n -> p e n").bitcast(I32))
+            for e in range(lo, hi):
+                held[e] = t[:, e - lo, :]
+
+        def load_fp8(t, words):
+            nc.sync.dma_start(out=t[:], in_=words[0].rearrange("p n d -> p (n d)").bitcast(I32))
+
+        nc.sync.dma_start(offs_t[:], offs)
+        load_scales(nc.sync, range(0, 4), (xs[:], x_scales))
+        load_fp8(xw, x_words)
+        load_fp4(w1_words, w1, "w1", 0, 1)
+        load_scales(nc.sync, range(0, 4), (s1[:], w1_scales[:, 0]))
+        load_fp4(w3_words, w3, "w3", 0, 1)
+        load_scales(nc.sync, range(0, 4), (s3[:], w3_scales[:, 0]))
+        load_fp4(w1_words, w1, "w1", 1, 2)
+        load_fp4(w3_words, w3, "w3", 1, 2)
+        load_scales(nc.gpsimd, range(0, 4), (s2[:], w2_scales[:, 0]))
+        load_fp4(w1_words, w1, "w1", 2, 4)
+        load_fp4(w3_words, w3, "w3", 2, 4)
+        load_fp4(w2_words, w2, "w2", 0, 6)
+        load_scales(nc.gpsimd, range(0, 4), (s3s[:], w3s_scales))
+        load_fp4(w1_words, w1, "w1", 4, 6)
+        load_fp4(w3_words, w3, "w3", 4, 6)
+        load_scales(nc.sync, range(0, 4), (s1s[:], w1s_scales))
+        load_fp8(w1s, w1s_words)
+        load_fp8(w3s, w3s_words)
+        load_scales(nc.gpsimd, range(0, 4), (s2s[:], w2s_scales))
+        load_fp8(w2s, w2s_words)
+        nc.sync.dma_start(pos1_t[:], pos1)
+        nc.sync.dma_start(pos2_t[:], pos2)
+        nc.sync.dma_start(out=gate_t[:], in_=gate.rearrange("r p t -> p r t"))
+
+        y = [keep.tile([P, S], F32, name="y%d" % v) for v in range(2)]
+        banks = [psum.tile([P, H], F32, name="bank%d" % k) for k in range(8)]
+        got_words = ring("gw", HELD_WORDS, [P, C], U32)
+        got_scales = ring("gs", HELD_SCALES, [P, C], U8)
+        acts = ring("act", 4, [P, 2, P, 2], F32)
+        hidden = ring("h", 6, [P, 2, P, 2], BF16)
+        turned = ring("ht", 2, [P, 4 * G], BF16)
+        codes = ring("hq", len(ORDER), [P, G], U32)
+        code_scales = ring("hs", len(ORDER), [P, G], U8)
+
+        def gather(e, into, window):
+            nc.vector.tensor_copy(into[e % len(into)][:], window.indirect(offs_t[:, e * C // 16 : (e + 1) * C // 16]))
+
+        def first_layer(i, where):
+            g = ORDER[i]
+            if g < E:
+                words, scales = got_words[g % HELD_WORDS][:], got_scales[g % HELD_SCALES][:]
+                sides = ((w1[g].bitcast(FP4X4), s1[:, g, :]), (w3[g].bitcast(FP4X4), s3[:, g, :]))
+            else:
+                words, scales = xw[:, (g - E) * G : (g - E + 1) * G], xs[:, 0, (g - E) * G : (g - E + 1) * G]
+                sides = ((w1s[:].bitcast(FP8X4), s1s[:, 0, :]), (w3s[:].bitcast(FP8X4), s3s[:, 0, :]))
+            for j in range(2):
+                cols = slice(j * P, (j + 1) * P)
+                k = 2 * i + j
+                a, b = banks[where[j]], banks[where[2 + j]]
+                for acc, (w, ws) in zip((a, b), sides):
+                    nc.tensor.matmul_mx(
+                        out=acc[:], lhsT=words[:, cols].bitcast(FP8X4), lhsT_scale=scales[:, cols],
+                        rhs=w, rhs_scale=ws, start=True, stop=True,
+                    )
+                act = acts[k % len(acts)]
+                nc.scalar.activation(act[:], a[:].rearrange("p (m u e) -> p u m e", u=2, e=2), GELU)
+                nc.vector.tensor_tensor(
+                    hidden[k % len(hidden)][:], b[:].rearrange("p (m u e) -> p u m e", u=2, e=2), act[:], MULT
+                )
+
+        def turn(i, bank, copy):
+            tr = bank[:].rearrange("p (j u r) -> p j u r", j=2, u=2)
+            for j in range(2):
+                pairs = hidden[(2 * i + j) % len(hidden)][:].rearrange("p u m e -> p (u m e)").bitcast(F32)
+                for u in range(2):
+                    nc.tensor.transpose(tr[:, j, u, :], pairs[:, u * P : (u + 1) * P], ident[:])
+            ht = turned[i % 2]
+            copy(
+                ht[:].bitcast(F32).rearrange("p (j r u) -> p j r u", j=2, u=2), tr.rearrange("p j u r -> p j r u")
+            )
+            nc.vector.quantize_mx(out=codes[i][:].bitcast(FP8X4), scales=code_scales[i][:], in_=ht[:])
+
+        def second_layer(i, sums, copy):
+            g = ORDER[i]
+            for v in range(2):
+                cols = slice(v * P, (v + 1) * P)
+                if g < E:
+                    w, ws = w2[g][:, 2 * v * P : 2 * (v + 1) * P].bitcast(FP4X4), s2[:, g, cols]
+                else:
+                    w, ws = w2s[:, cols].bitcast(FP8X4), s2s[:, 0, cols]
+                nc.tensor.matmul_mx(
+                    out=sums[v], lhsT=w, lhsT_scale=ws, rhs=codes[i][:].bitcast(FP8X4), rhs_scale=code_scales[i][:],
+                    start=True, stop=True,
+                )
+            if g < E:
+                for v in range(2):
+                    copy(y[v][:, g * C : (g + 1) * C], sums[v])
+
+        wide = [banks[3], banks[0]]
+        last = banks[1]
+        for kind, i, bank, engine in STEPS:
+            copy = nc.vector.tensor_copy if engine == "v" else nc.scalar.copy
+            if kind == "words":
+                gather(i, got_words, xw[:].bitcast(U32))
+            elif kind == "scales":
+                gather(i, got_scales, xs[:, 0, :])
+            elif kind == "first":
+                first_layer(i, bank)
+            elif kind == "turn":
+                turn(i, banks[bank], copy)
+            elif ORDER[i] < E:
+                second_layer(i, [banks[bank][:, v * G : (v + 1) * G] for v in range(2)], copy)
+            elif ORDER[i] < E + 2:
+                c = ORDER[i] - E
+                second_layer(i, [wide[v][:, c * G : (c + 1) * G] for v in range(2)], copy)
+            else:
+                second_layer(i, [last[:, v * G : (v + 1) * G] for v in range(2)], copy)
+
+        first = [keep.tile([P, T], F32, name="first%d" % v) for v in range(2)]
+        second = [keep.tile([P, T], F32, name="second%d" % v) for v in range(2)]
+        part = [keep.tile([P, T], F32, name="part%d" % v) for v in range(2)]
+        res = [keep.tile([P, T], F32, name="res%d" % v) for v in range(2)]
+        for v in range(2):
+            nc.vector.tensor_tensor(first[v][:], y[v][:].indirect(pos1_t[:]), gate_t[:, 0, :], MULT)
+        for v in range(2):
+            nc.vector.tensor_tensor(part[v][:, 0 : 2 * G], wide[v][:], first[v][:, 0 : 2 * G], ADD)
+            nc.vector.tensor_tensor(part[v][:, 2 * G : T], last[:, v * G : (v + 1) * G], first[v][:, 2 * G : T], ADD)
+        for v in range(2):
+            nc.vector.tensor_tensor(second[v][:], y[v][:].indirect(pos2_t[:]), gate_t[:, 1, :], MULT)
+            nc.vector.tensor_tensor(res[v][:], part[v][:], second[v][:], ADD)
+            nc.sync.dma_start(out=out[v * P : (v + 1) * P, :], in_=res[v][:])

@@ -21,10 +21,10 @@ ADD = mybir.AluOpType.add
 
 P = 128
 G = 256
-HELD_WORDS = 4
-HELD_SCALES = 2
+HELD_WORDS = 6
+HELD_SCALES = 4
 ORDER = [0, 1, 2, 3, 4, 5, 6, 7, 8]
-STEPS = [["words",2,0,"a"],["words",0,0,"a"],["words",3,0,"a"],["words",1,0,"a"],["scales",1,0,"a"],["scales",0,0,"a"],["first",0,[6,1,4,3],"a"],["scales",2,0,"a"],["first",1,[2,5,6,0],"a"],["scales",3,0,"a"],["first",2,[3,6,0,5],"a"],["turn",1,7,"a"],["scales",4,0,"a"],["turn",0,4,"a"],["words",4,0,"a"],["first",3,[2,3,4,7],"a"],["scales",5,0,"a"],["second",1,1,"a"],["turn",2,5,"a"],["words",5,0,"a"],["second",2,3,"v"],["first",4,[2,0,4,5],"a"],["second",0,6,"a"],["turn",3,6,"a"],["first",5,[1,2,6,7],"a"],["turn",4,5,"v"],["first",6,[0,1,4,5],"a"],["turn",5,6,"v"],["second",3,3,"a"],["first",7,[2,0,6,7],"a"],["first",8,[1,7,3,5],"a"],["second",4,4,"a"],["turn",7,1,"a"],["turn",6,3,"a"],["turn",8,1,"a"],["second",8,0,"a"],["second",6,0,"a"],["second",7,0,"a"],["second",5,2,"a"]]
+STEPS = [["words",0,1,"a"],["scales",0,2,"a"],["words",1,1,"a"],["first",0,[5,0,4,7],"a"],["first",1,[6,2,5,1],"a"],["words",2,2,"a"],["turn",1,0,"a"],["scales",2,2,"a"],["turn",0,4,"a"],["first",2,[6,7,1,5],"a"],["scales",4,2,"a"],["turn",2,7,"a"],["first",3,[0,2,5,4],"a"],["words",4,2,"a"],["second",0,6,"v"],["first",5,[2,1,6,3],"a"],["first",4,[1,2,4,7],"a"],["second",2,3,"v"],["turn",3,5,"a"],["turn",5,4,"v"],["first",6,[2,1,4,6],"a"],["second",1,7,"a"],["turn",4,5,"a"],["first",7,[7,0,6,2],"a"],["first",8,[0,1,5,7],"a"],["second",4,4,"a"],["second",3,2,"a"],["turn",6,1,"a"],["turn",7,2,"a"],["second",6,5,"a"],["second",7,0,"a"],["turn",8,6,"a"],["second",5,3,"a"],["second",8,0,"a"]]
 
 
 def load_scales(queue, quadrants, *pairs):
@@ -83,25 +83,23 @@ def tile_moe_shf_glu_gelu_kernel(
             nc.sync.dma_start(out=t[:], in_=words[0].rearrange("p n d -> p (n d)").bitcast(I32))
 
         nc.sync.dma_start(offs_t[:], offs)
-        load_scales(nc.sync, range(0, 4), (xs[:], x_scales))
+        load_scales(nc.sync, (0, 2, 1, 3), (xs[:], x_scales))
         load_fp8(xw, x_words)
-        load_fp4(w1_words, w1, "w1", 0, 1)
-        load_scales(nc.sync, range(0, 4), (s1[:], w1_scales[:, 0]))
-        load_fp4(w3_words, w3, "w3", 0, 1)
-        load_scales(nc.sync, range(0, 4), (s3[:], w3_scales[:, 0]))
-        load_fp4(w1_words, w1, "w1", 1, 2)
-        load_fp4(w3_words, w3, "w3", 1, 2)
-        load_scales(nc.gpsimd, range(0, 4), (s2[:], w2_scales[:, 0]))
+        load_fp4(w1_words, w1, "w1", 0, 2)
+        load_scales(nc.sync, (0, 2, 1, 3), (s1[:], w1_scales[:, 0]))
+        load_fp4(w3_words, w3, "w3", 0, 2)
+        load_scales(nc.sync, (0, 2, 1, 3), (s3[:], w3_scales[:, 0]))
+        load_scales(nc.gpsimd, (0, 2, 1, 3), (s2[:], w2_scales[:, 0]))
         load_fp4(w1_words, w1, "w1", 2, 4)
         load_fp4(w3_words, w3, "w3", 2, 4)
         load_fp4(w2_words, w2, "w2", 0, 6)
-        load_scales(nc.gpsimd, range(0, 4), (s3s[:], w3s_scales))
+        load_scales(nc.gpsimd, (0, 2, 1, 3), (s3s[:], w3s_scales))
         load_fp4(w1_words, w1, "w1", 4, 6)
         load_fp4(w3_words, w3, "w3", 4, 6)
-        load_scales(nc.sync, range(0, 4), (s1s[:], w1s_scales))
+        load_scales(nc.sync, (0, 2, 1, 3), (s1s[:], w1s_scales))
         load_fp8(w1s, w1s_words)
         load_fp8(w3s, w3s_words)
-        load_scales(nc.gpsimd, range(0, 4), (s2s[:], w2s_scales))
+        load_scales(nc.gpsimd, (0, 2, 1, 3), (s2s[:], w2s_scales))
         load_fp8(w2s, w2s_words)
         nc.sync.dma_start(pos1_t[:], pos1)
         nc.sync.dma_start(pos2_t[:], pos2)
@@ -109,21 +107,25 @@ def tile_moe_shf_glu_gelu_kernel(
 
         y = [keep.tile([P, S], F32, name="y%d" % v) for v in range(2)]
         banks = [psum.tile([P, H], F32, name="bank%d" % k) for k in range(8)]
-        got_words = ring("gw", HELD_WORDS, [P, C], U32)
-        got_scales = ring("gs", HELD_SCALES, [P, C], U8)
-        acts = ring("act", 4, [P, 2, P, 2], F32)
-        hidden = ring("h", 6, [P, 2, P, 2], BF16)
+        got_words = keep.tile([P, HELD_WORDS, C], U32, name="got_words", align_bytes=64)
+        got_scales = keep.tile([P, HELD_SCALES, C], U8, name="got_scales", align_bytes=64)
+        acts = ring("act", 8, [P, 2, P, 2], F32)
+        hidden = ring("h", 8, [P, 2, P, 2], BF16)
         turned = ring("ht", 2, [P, 4 * G], BF16)
         codes = ring("hq", len(ORDER), [P, G], U32)
         code_scales = ring("hs", len(ORDER), [P, G], U8)
 
-        def gather(e, into, window):
-            nc.vector.tensor_copy(into[e % len(into)][:], window.indirect(offs_t[:, e * C // 16 : (e + 1) * C // 16]))
+        def gather(e, count, into, window):
+            slot = e % into.shape[1]
+            nc.vector.tensor_copy(
+                into[:, slot : slot + count, :].rearrange("p e c -> p (e c)"),
+                window.indirect(offs_t[:, e * C // 16 : (e + count) * C // 16]),
+            )
 
         def first_layer(i, where):
             g = ORDER[i]
             if g < E:
-                words, scales = got_words[g % HELD_WORDS][:], got_scales[g % HELD_SCALES][:]
+                words, scales = got_words[:, g % HELD_WORDS, :], got_scales[:, g % HELD_SCALES, :]
                 sides = ((w1[g].bitcast(FP4X4), s1[:, g, :]), (w3[g].bitcast(FP4X4), s3[:, g, :]))
             else:
                 words, scales = xw[:, (g - E) * G : (g - E + 1) * G], xs[:, 0, (g - E) * G : (g - E + 1) * G]
@@ -171,14 +173,14 @@ def tile_moe_shf_glu_gelu_kernel(
                 for v in range(2):
                     copy(y[v][:, g * C : (g + 1) * C], sums[v])
 
-        wide = [banks[3], banks[0]]
         last = banks[1]
+        shared = [keep.tile([P, 2, N], F32, name="shared%d" % c) for c in range(2)]
         for kind, i, bank, engine in STEPS:
             copy = nc.vector.tensor_copy if engine == "v" else nc.scalar.copy
             if kind == "words":
-                gather(i, got_words, xw[:].bitcast(U32))
+                gather(i, bank, got_words, xw[:].bitcast(U32))
             elif kind == "scales":
-                gather(i, got_scales, xs[:, 0, :])
+                gather(i, bank, got_scales, xs[:, 0, :])
             elif kind == "first":
                 first_layer(i, bank)
             elif kind == "turn":
@@ -186,21 +188,53 @@ def tile_moe_shf_glu_gelu_kernel(
             elif ORDER[i] < E:
                 second_layer(i, [banks[bank][:, v * G : (v + 1) * G] for v in range(2)], copy)
             elif ORDER[i] < E + 2:
-                c = ORDER[i] - E
-                second_layer(i, [wide[v][:, c * G : (c + 1) * G] for v in range(2)], copy)
+                for j in range(2):
+                    nc.tensor.matmul_mx(
+                        out=banks[bank][:, j * N : (j + 1) * N],
+                        lhsT=codes[i][:, j * P : (j + 1) * P].bitcast(FP8X4),
+                        lhsT_scale=code_scales[i][:, j * P : (j + 1) * P],
+                        rhs=w2s[:].bitcast(FP8X4), rhs_scale=s2s[:, 0, :], start=True, stop=True,
+                    )
+                copy(shared[ORDER[i] - E][:].rearrange("p j n -> p (j n)"), banks[bank][:])
             else:
                 second_layer(i, [last[:, v * G : (v + 1) * G] for v in range(2)], copy)
 
-        first = [keep.tile([P, T], F32, name="first%d" % v) for v in range(2)]
-        second = [keep.tile([P, T], F32, name="second%d" % v) for v in range(2)]
-        part = [keep.tile([P, T], F32, name="part%d" % v) for v in range(2)]
-        res = [keep.tile([P, T], F32, name="res%d" % v) for v in range(2)]
+        def pick(into, v, places, r, c):
+            nc.vector.tensor_tensor(
+                into, y[v][:].indirect(places[:, c * G // 16 : (c + 1) * G // 16]), gate_t[:, r, c * G : (c + 1) * G], MULT
+            )
+
+        def turn_and_add(into, terms):
+            for k, term in enumerate(terms):
+                nc.tensor.matmul(into, term, ident[:], start=(k == 0), stop=(k == len(terms) - 1), is_transpose=True)
+
+        blocks = [slice(j * P, (j + 1) * P) for j in range(2)]
+        for u, (sum_bank, back_bank) in enumerate(((4, 5), (6, 7), (0, 2), (3, 4))):
+            c, v = divmod(u, 2)
+            first, second, by_token, res = (
+                keep.tile([P, G], F32, name="%s%d" % (name, u)) for name in ("first", "second", "by_token", "res")
+            )
+            pick(first[:], v, pos1_t, 0, c)
+            pick(second[:], v, pos2_t, 1, c)
+            for block in blocks:
+                turn_and_add(banks[sum_bank][:, block], (first[:, block], second[:, block]))
+            nc.scalar.copy(by_token[:], banks[sum_bank][:, 0:G])
+            for j, block in enumerate(blocks):
+                turn_and_add(banks[back_bank][:, block], (shared[c][:, j, v * P : (v + 1) * P], by_token[:, block]))
+            nc.scalar.copy(res[:], banks[back_bank][:, 0:G])
+            nc.sync.dma_start(out=out[v * P : (v + 1) * P, c * G : (c + 1) * G], in_=res[:])
+
+        c = 2
+        first, second, part, res = (
+            keep.tile([P, 2, G], F32, name="late_" + name) for name in ("first", "second", "part", "res")
+        )
         for v in range(2):
-            nc.vector.tensor_tensor(first[v][:], y[v][:].indirect(pos1_t[:]), gate_t[:, 0, :], MULT)
+            pick(first[:, v, :], v, pos1_t, 0, c)
+        pick(second[:, 0, :], 0, pos2_t, 1, c)
+        nc.vector.tensor_tensor(
+            part[:].rearrange("p v t -> p (v t)"), last[:], first[:].rearrange("p v t -> p (v t)"), ADD
+        )
+        pick(second[:, 1, :], 1, pos2_t, 1, c)
         for v in range(2):
-            nc.vector.tensor_tensor(part[v][:, 0 : 2 * G], wide[v][:], first[v][:, 0 : 2 * G], ADD)
-            nc.vector.tensor_tensor(part[v][:, 2 * G : T], last[:, v * G : (v + 1) * G], first[v][:, 2 * G : T], ADD)
-        for v in range(2):
-            nc.vector.tensor_tensor(second[v][:], y[v][:].indirect(pos2_t[:]), gate_t[:, 1, :], MULT)
-            nc.vector.tensor_tensor(res[v][:], part[v][:], second[v][:], ADD)
-            nc.sync.dma_start(out=out[v * P : (v + 1) * P, :], in_=res[v][:])
+            nc.vector.tensor_tensor(res[:, v, :], part[:, v, :], second[:, v, :], ADD)
+            nc.sync.dma_start(out=out[v * P : (v + 1) * P, c * G : (c + 1) * G], in_=res[:, v, :])

@@ -24,7 +24,7 @@ G = 256
 HELD_WORDS = 6
 HELD_SCALES = 4
 ORDER = [0, 1, 2, 3, 4, 5, 6, 7, 8]
-STEPS = [["words",0,1,"a"],["scales",0,2,"a"],["words",1,1,"a"],["first",0,[5,0,4,7],"a"],["first",1,[6,2,5,1],"a"],["words",2,2,"a"],["turn",1,0,"a"],["scales",2,2,"a"],["turn",0,4,"a"],["first",2,[6,7,1,5],"a"],["scales",4,2,"a"],["turn",2,7,"a"],["first",3,[0,2,5,4],"a"],["words",4,2,"a"],["second",0,6,"v"],["first",5,[2,1,6,3],"a"],["first",4,[1,2,4,7],"a"],["second",2,3,"v"],["turn",3,5,"a"],["turn",5,4,"v"],["first",6,[2,1,4,6],"a"],["second",1,7,"a"],["turn",4,5,"a"],["first",7,[7,0,6,2],"a"],["first",8,[0,1,5,7],"a"],["second",4,4,"a"],["second",3,2,"a"],["turn",6,1,"a"],["turn",7,2,"a"],["second",6,5,"a"],["second",7,0,"a"],["turn",8,6,"a"],["second",5,3,"a"],["second",8,0,"a"]]
+STEPS = [["words",0,1,"a"],["scales",0,2,"a"],["first",0,[5,6,4,7],"a"],["scales",2,2,"a"],["words",1,1,"a"],["turn",0,4,"a"],["words",2,2,"a"],["first",1,[0,2,5,1],"a"],["first",2,[6,7,1,5],"a"],["turn",2,7,"a"],["first",3,[0,3,5,4],"a"],["scales",4,2,"a"],["words",4,2,"a"],["first",4,[1,3,4,7],"a"],["turn",1,0,"a"],["turn",3,5,"a"],["turn",4,5,"v"],["first",5,[2,1,6,0],"a"],["turn",5,4,"a"],["second",0,6,"a"],["second",2,3,"a"],["second",1,7,"v"],["second",4,3,"a"],["first",6,[2,1,4,6],"a"],["first",7,[7,0,6,1],"a"],["second",5,7,"a"],["second",3,2,"a"],["first",8,[0,2,5,1],"a"],["turn",7,3,"a"],["turn",6,4,"a"],["turn",8,3,"a"],["second",6,1,"a"],["second",7,7,"a"],["second",8,0,"a"]]
 
 
 def load_scales(queue, quadrants, *pairs):
@@ -83,7 +83,8 @@ def tile_moe_shf_glu_gelu_kernel(
             nc.sync.dma_start(out=t[:], in_=words[0].rearrange("p n d -> p (n d)").bitcast(I32))
 
         nc.sync.dma_start(offs_t[:], offs)
-        load_scales(nc.sync, (0, 2, 1, 3), (xs[:], x_scales))
+        load_scales(nc.sync, range(0, 2), (xs[:], x_scales))
+        load_scales(nc.scalar, range(2, 4), (xs[:], x_scales))
         load_fp8(xw, x_words)
         load_fp4(w1_words, w1, "w1", 0, 2)
         load_scales(nc.sync, (0, 2, 1, 3), (s1[:], w1_scales[:, 0]))

@@ -21,19 +21,15 @@ ADD = mybir.AluOpType.add
 
 P = 128
 G = 256
-HELD_WORDS = 6
-HELD_SCALES = 4
-ORDER = [0, 1, 2, 3, 4, 5, 6, 7, 8]
-STEPS = [["words",0,1,"a"],["scales",0,2,"a"],["first",0,[5,6,4,7],"a"],["scales",2,2,"a"],["words",1,1,"a"],["turn",0,4,"a"],["words",2,2,"a"],["first",1,[0,2,5,1],"a"],["first",2,[6,7,1,5],"a"],["turn",2,7,"a"],["first",3,[0,3,5,4],"a"],["scales",4,2,"a"],["words",4,2,"a"],["first",4,[1,3,4,7],"a"],["turn",1,0,"a"],["turn",3,5,"a"],["turn",4,5,"v"],["first",5,[2,1,6,0],"a"],["turn",5,4,"a"],["second",0,6,"a"],["second",2,3,"a"],["second",1,7,"v"],["second",4,3,"a"],["first",6,[2,1,4,6],"a"],["first",7,[7,0,6,1],"a"],["second",5,7,"a"],["second",3,2,"a"],["first",8,[0,2,5,1],"a"],["turn",7,3,"a"],["turn",6,4,"a"],["turn",8,3,"a"],["second",6,1,"a"],["second",7,7,"a"],["second",8,0,"a"]]
+GROUPS = E + T // G
 
 
-def load_scales(queue, quadrants, *pairs):
+def load_scales(queue, quadrants, plane, scales):
     for q in quadrants:
-        for plane, scales in pairs:
-            queue.dma_start(
-                out=plane[32 * q : 32 * q + 4, :, :].bitcast(I32),
-                in_=scales[:, 4 * q : 4 * q + 4, :].rearrange("m r w -> r m w").bitcast(I32),
-            )
+        queue.dma_start(
+            out=plane[32 * q : 32 * q + 4, :, :].bitcast(I32),
+            in_=scales[:, 4 * q : 4 * q + 4, :].rearrange("m r w -> r m w").bitcast(I32),
+        )
 
 
 def tile_moe_shf_glu_gelu_kernel(
@@ -45,7 +41,7 @@ def tile_moe_shf_glu_gelu_kernel(
         keep = ctx.enter_context(tc.tile_pool(name="keep", bufs=1))
         psum = ctx.enter_context(tc.psum_pool(name="psum", bufs=1))
 
-        def ring(name, count, shape, dtype):
+        def tiles(name, count, shape, dtype):
             return [keep.tile(shape, dtype, name="%s%d" % (name, k), align_bytes=64) for k in range(count)]
 
         offs_t = keep.tile([P, S // 16], U16, name="offs_t")
@@ -65,140 +61,160 @@ def tile_moe_shf_glu_gelu_kernel(
         gate_t = keep.tile([P, 2, T], F32, name="gate_t")
         ident = keep.tile([P, P], F32, name="ident")
 
-        for plane in (xs,):
+        for plane in (xs, s1s, s3s, s2s):
             nc.gpsimd.memset(plane[:].bitcast(I32), 0)
-        for plane in (s1, s3, s2, s1s, s3s, s2s):
+        for plane in (s1, s3, s2):
             nc.vector.memset(plane[:].bitcast(I32), 0)
         make_identity(nc, ident[:])
 
         w1, w3, w2 = {}, {}, {}
 
-        def load_fp4(words, held, name, lo, hi):
+        def load_fp4(queue, words, held, name, lo, hi):
             t = keep.tile([P, hi - lo, words.shape[3]], U8, name="%s_%d" % (name, lo), align_bytes=64)
-            nc.sync.dma_start(out=t[:].bitcast(I32), in_=words[lo:hi, 0].rearrange("e p n -> p e n").bitcast(I32))
+            queue.dma_start(out=t[:].bitcast(I32), in_=words[lo:hi, 0].rearrange("e p n -> p e n").bitcast(I32))
             for e in range(lo, hi):
                 held[e] = t[:, e - lo, :]
 
-        def load_fp8(t, words):
-            nc.sync.dma_start(out=t[:], in_=words[0].rearrange("p n d -> p (n d)").bitcast(I32))
+        def load_fp8(queue, t, words):
+            queue.dma_start(out=t[:], in_=words[0].rearrange("p n d -> p (n d)").bitcast(I32))
 
+        ports = (0, 2, 1, 3)
+        def load_tokens(half):
+            nc.sync.dma_start(out=xw[:, half], in_=x_words[0, :, half].rearrange("p n d -> p (n d)").bitcast(I32))
+
+        load_tokens(slice(0, T // 2))
+        load_scales(nc.sync, (0,), xs[:], x_scales)
+        load_scales(nc.scalar, (2, 1, 3), xs[:], x_scales)
+        load_tokens(slice(T // 2, T))
         nc.sync.dma_start(offs_t[:], offs)
-        load_scales(nc.sync, range(0, 2), (xs[:], x_scales))
-        load_scales(nc.scalar, range(2, 4), (xs[:], x_scales))
-        load_fp8(xw, x_words)
-        load_fp4(w1_words, w1, "w1", 0, 2)
-        load_scales(nc.sync, (0, 2, 1, 3), (s1[:], w1_scales[:, 0]))
-        load_fp4(w3_words, w3, "w3", 0, 2)
-        load_scales(nc.sync, (0, 2, 1, 3), (s3[:], w3_scales[:, 0]))
-        load_scales(nc.gpsimd, (0, 2, 1, 3), (s2[:], w2_scales[:, 0]))
-        load_fp4(w1_words, w1, "w1", 2, 4)
-        load_fp4(w3_words, w3, "w3", 2, 4)
-        load_fp4(w2_words, w2, "w2", 0, 6)
-        load_scales(nc.gpsimd, (0, 2, 1, 3), (s3s[:], w3s_scales))
-        load_fp4(w1_words, w1, "w1", 4, 6)
-        load_fp4(w3_words, w3, "w3", 4, 6)
-        load_scales(nc.sync, (0, 2, 1, 3), (s1s[:], w1s_scales))
-        load_fp8(w1s, w1s_words)
-        load_fp8(w3s, w3s_words)
-        load_scales(nc.gpsimd, (0, 2, 1, 3), (s2s[:], w2s_scales))
-        load_fp8(w2s, w2s_words)
+        load_fp4(nc.sync, w1_words, w1, "w1", 0, 1)
+        load_scales(nc.scalar, (1, 3), s1[:], w1_scales[:, 0])
+        load_scales(nc.sync, (0, 2), s1[:], w1_scales[:, 0])
+        load_scales(nc.gpsimd, (1, 3), s3[:], w3_scales[:, 0])
+        load_fp4(nc.sync, w1_words, w1, "w1", 1, 4)
+        load_fp4(nc.sync, w1_words, w1, "w1", 4, 6)
+        load_fp4(nc.sync, w3_words, w3, "w3", 0, 2)
+        load_scales(nc.sync, (0, 2), s3[:], w3_scales[:, 0])
+        load_fp8(nc.sync, w1s, w1s_words)
+        load_scales(nc.gpsimd, (1, 3), s2[:], w2_scales[:, 0])
+        load_scales(nc.gpsimd, ports, s1s[:], w1s_scales)
+        load_fp4(nc.sync, w3_words, w3, "w3", 2, 4)
+        load_scales(nc.sync, (0, 2), s2[:], w2_scales[:, 0])
+        load_fp4(nc.sync, w2_words, w2, "w2", 0, 6)
+        load_fp4(nc.sync, w3_words, w3, "w3", 4, 6)
+        load_fp8(nc.sync, w3s, w3s_words)
+        load_scales(nc.sync, ports, s3s[:], w3s_scales)
+        load_scales(nc.gpsimd, ports, s2s[:], w2s_scales)
+        load_fp8(nc.sync, w2s, w2s_words)
         nc.sync.dma_start(pos1_t[:], pos1)
         nc.sync.dma_start(pos2_t[:], pos2)
         nc.sync.dma_start(out=gate_t[:], in_=gate.rearrange("r p t -> p r t"))
 
         y = [keep.tile([P, S], F32, name="y%d" % v) for v in range(2)]
         banks = [psum.tile([P, H], F32, name="bank%d" % k) for k in range(8)]
-        got_words = keep.tile([P, HELD_WORDS, C], U32, name="got_words", align_bytes=64)
-        got_scales = keep.tile([P, HELD_SCALES, C], U8, name="got_scales", align_bytes=64)
-        acts = ring("act", 8, [P, 2, P, 2], F32)
-        hidden = ring("h", 8, [P, 2, P, 2], BF16)
-        turned = ring("ht", 2, [P, 4 * G], BF16)
-        codes = ring("hq", len(ORDER), [P, G], U32)
-        code_scales = ring("hs", len(ORDER), [P, G], U8)
+        first_banks, turn_bank, sum_bank = banks[0:6], banks[6], banks[7]
+        got_words, got_scales = {}, {}
+        acts = tiles("act", 2 * GROUPS, [P, 2, P, 2], F32)
+        hidden = tiles("h", 2 * GROUPS, [P, 2, P, 2], BF16)
+        turned = tiles("ht", GROUPS, [P, 4 * G], BF16)
+        codes = tiles("hq", GROUPS, [P, G], U32)
+        code_scales = tiles("hs", GROUPS, [P, G], U8)
+        shared = tiles("shared", 3, [P, 2, N], F32)
 
-        def gather(e, count, into, window):
-            slot = e % into.shape[1]
-            nc.vector.tensor_copy(
-                into[:, slot : slot + count, :].rearrange("p e c -> p (e c)"),
-                window.indirect(offs_t[:, e * C // 16 : (e + count) * C // 16]),
-            )
+        def gather(e, count):
+            for held, window, name in ((got_scales, xs[:, 0, :], "got_scales"), (got_words, xw[:].bitcast(U32), "got_words")):
+                into = keep.tile([P, count * C], window.dtype, name="%s%d" % (name, e), align_bytes=64)
+                nc.vector.tensor_copy(into[:], window.indirect(offs_t[:, e * C // 16 : (e + count) * C // 16]))
+                for i in range(count):
+                    held[e + i] = into[:, i * C : (i + 1) * C]
 
-        def first_layer(i, where):
-            g = ORDER[i]
+        def first_product(acc, k, routed, routed_scales, common, common_scales):
+            g, j = divmod(k, 2)
+            cols = slice(j * P, (j + 1) * P)
             if g < E:
-                words, scales = got_words[:, g % HELD_WORDS, :], got_scales[:, g % HELD_SCALES, :]
-                sides = ((w1[g].bitcast(FP4X4), s1[:, g, :]), (w3[g].bitcast(FP4X4), s3[:, g, :]))
+                words, scales = got_words[g][:, cols], got_scales[g][:, cols]
+                w, ws = routed[g].bitcast(FP4X4), routed_scales[:, g, :]
             else:
-                words, scales = xw[:, (g - E) * G : (g - E + 1) * G], xs[:, 0, (g - E) * G : (g - E + 1) * G]
-                sides = ((w1s[:].bitcast(FP8X4), s1s[:, 0, :]), (w3s[:].bitcast(FP8X4), s3s[:, 0, :]))
-            for j in range(2):
-                cols = slice(j * P, (j + 1) * P)
-                k = 2 * i + j
-                a, b = banks[where[j]], banks[where[2 + j]]
-                for acc, (w, ws) in zip((a, b), sides):
-                    nc.tensor.matmul_mx(
-                        out=acc[:], lhsT=words[:, cols].bitcast(FP8X4), lhsT_scale=scales[:, cols],
-                        rhs=w, rhs_scale=ws, start=True, stop=True,
-                    )
-                act = acts[k % len(acts)]
-                nc.scalar.activation(act[:], a[:].rearrange("p (m u e) -> p u m e", u=2, e=2), GELU)
-                nc.vector.tensor_tensor(
-                    hidden[k % len(hidden)][:], b[:].rearrange("p (m u e) -> p u m e", u=2, e=2), act[:], MULT
-                )
+                cols = slice((k - 2 * E) * P, (k - 2 * E + 1) * P)
+                words, scales = xw[:, cols], xs[:, 0, cols]
+                w, ws = common[:].bitcast(FP8X4), common_scales[:, 0, :]
+            nc.tensor.matmul_mx(
+                out=acc[:], lhsT=words.bitcast(FP8X4), lhsT_scale=scales, rhs=w, rhs_scale=ws, start=True, stop=True
+            )
+            return acc[:].rearrange("p (m u e) -> p u m e", u=2, e=2)
 
-        def turn(i, bank, copy):
-            tr = bank[:].rearrange("p (j u r) -> p j u r", j=2, u=2)
+        def gelu_side(k, bank):
+            sums = first_product(bank, k, w1, s1, w1s, s1s)
+            nc.scalar.activation(acts[k][:], sums, GELU)
+
+        def gate_side(k, bank):
+            sums = first_product(bank, k, w3, s3, w3s, s3s)
+            nc.vector.tensor_tensor(hidden[k][:], sums, acts[k][:], MULT)
+
+        def turn(g):
+            tr = turn_bank[:].rearrange("p (j u r) -> p j u r", j=2, u=2)
             for j in range(2):
-                pairs = hidden[(2 * i + j) % len(hidden)][:].rearrange("p u m e -> p (u m e)").bitcast(F32)
+                pairs = hidden[2 * g + j][:].rearrange("p u m e -> p (u m e)").bitcast(F32)
                 for u in range(2):
                     nc.tensor.transpose(tr[:, j, u, :], pairs[:, u * P : (u + 1) * P], ident[:])
-            ht = turned[i % 2]
-            copy(
+            ht = turned[g]
+            nc.scalar.copy(
                 ht[:].bitcast(F32).rearrange("p (j r u) -> p j r u", j=2, u=2), tr.rearrange("p j u r -> p j r u")
             )
-            nc.vector.quantize_mx(out=codes[i][:].bitcast(FP8X4), scales=code_scales[i][:], in_=ht[:])
 
-        def second_layer(i, sums, copy):
-            g = ORDER[i]
+        def quantise(g):
+            nc.vector.quantize_mx(out=codes[g][:].bitcast(FP8X4), scales=code_scales[g][:], in_=turned[g][:])
+
+        def by_feature(acc, g, w, ws):
+            nc.tensor.matmul_mx(
+                out=acc, lhsT=w, lhsT_scale=ws, rhs=codes[g][:].bitcast(FP8X4), rhs_scale=code_scales[g][:],
+                start=True, stop=True,
+            )
+
+        def second_routed(g):
             for v in range(2):
                 cols = slice(v * P, (v + 1) * P)
-                if g < E:
-                    w, ws = w2[g][:, 2 * v * P : 2 * (v + 1) * P].bitcast(FP4X4), s2[:, g, cols]
-                else:
-                    w, ws = w2s[:, cols].bitcast(FP8X4), s2s[:, 0, cols]
-                nc.tensor.matmul_mx(
-                    out=sums[v], lhsT=w, lhsT_scale=ws, rhs=codes[i][:].bitcast(FP8X4), rhs_scale=code_scales[i][:],
-                    start=True, stop=True,
-                )
-            if g < E:
-                for v in range(2):
-                    copy(y[v][:, g * C : (g + 1) * C], sums[v])
+                by_feature(sum_bank[:, v * G : (v + 1) * G], g, w2[g][:, 2 * v * P : 2 * (v + 1) * P].bitcast(FP4X4), s2[:, g, cols])
+            for v in range(2):
+                nc.scalar.copy(y[v][:, g * C : (g + 1) * C], sum_bank[:, v * G : (v + 1) * G])
 
-        last = banks[1]
-        shared = [keep.tile([P, 2, N], F32, name="shared%d" % c) for c in range(2)]
-        for kind, i, bank, engine in STEPS:
-            copy = nc.vector.tensor_copy if engine == "v" else nc.scalar.copy
-            if kind == "words":
-                gather(i, bank, got_words, xw[:].bitcast(U32))
-            elif kind == "scales":
-                gather(i, bank, got_scales, xs[:, 0, :])
-            elif kind == "first":
-                first_layer(i, bank)
-            elif kind == "turn":
-                turn(i, banks[bank], copy)
-            elif ORDER[i] < E:
-                second_layer(i, [banks[bank][:, v * G : (v + 1) * G] for v in range(2)], copy)
-            elif ORDER[i] < E + 2:
-                for j in range(2):
-                    nc.tensor.matmul_mx(
-                        out=banks[bank][:, j * N : (j + 1) * N],
-                        lhsT=codes[i][:, j * P : (j + 1) * P].bitcast(FP8X4),
-                        lhsT_scale=code_scales[i][:, j * P : (j + 1) * P],
-                        rhs=w2s[:].bitcast(FP8X4), rhs_scale=s2s[:, 0, :], start=True, stop=True,
-                    )
-                copy(shared[ORDER[i] - E][:].rearrange("p j n -> p (j n)"), banks[bank][:])
-            else:
-                second_layer(i, [last[:, v * G : (v + 1) * G] for v in range(2)], copy)
+        def second_shared(c, width):
+            for j in range(2):
+                nc.tensor.matmul_mx(
+                    out=sum_bank[:, j * N : j * N + width],
+                    lhsT=codes[E + c][:, j * P : (j + 1) * P].bitcast(FP8X4),
+                    lhsT_scale=code_scales[E + c][:, j * P : (j + 1) * P],
+                    rhs=w2s[:, 0:width].bitcast(FP8X4), rhs_scale=s2s[:, 0, 0:width], start=True, stop=True,
+                )
+            nc.scalar.copy(shared[c][:, :, 0:width], sum_bank[:].rearrange("p (j n) -> p j n", j=2)[:, :, 0:width])
+
+        for e in range(E):
+            gather(e, 1)
+        gelu_banks, gate_banks = first_banks[0:3], first_banks[3:6] + first_banks[0:1]
+        last = gelu_banks[1][:, 0:G]
+
+        def behind(g):
+            if 0 <= g < GROUPS:
+                turn(g)
+                quantise(g)
+            if 0 <= g - 1 < E:
+                second_routed(g - 1)
+            elif E <= g - 1 < GROUPS - 1:
+                second_shared(g - 1 - E, N)
+            elif g == GROUPS:
+                second_shared(g - 1 - E, P)
+                by_feature(last, g - 1, w2s[:, P:N].bitcast(FP8X4), s2s[:, 0, P:N])
+
+        for k in range(2 * E):
+            gelu_side(k, gelu_banks[k % 3])
+        for k in range(2 * GROUPS):
+            if 2 * E <= k + 2 < 2 * GROUPS:
+                gelu_side(k + 2, gelu_banks[1 + k % 2])
+            gate_side(k, gate_banks[k % 4])
+            if (k - 4) % 2 == 0:
+                behind((k - 4) // 2)
+        for g in range((2 * GROUPS - 4 + 1) // 2, GROUPS + 1):
+            behind(g)
 
         def pick(into, v, places, r, c):
             nc.vector.tensor_tensor(
@@ -209,33 +225,29 @@ def tile_moe_shf_glu_gelu_kernel(
             for k, term in enumerate(terms):
                 nc.tensor.matmul(into, term, ident[:], start=(k == 0), stop=(k == len(terms) - 1), is_transpose=True)
 
-        blocks = [slice(j * P, (j + 1) * P) for j in range(2)]
-        for u, (sum_bank, back_bank) in enumerate(((4, 5), (6, 7), (0, 2), (3, 4))):
+        def picked(u):
+            both = acts[2 * GROUPS - 2 + u % 2][:].rearrange("p u m e -> p (u m e)")
             c, v = divmod(u, 2)
-            first, second, by_token, res = (
-                keep.tile([P, G], F32, name="%s%d" % (name, u)) for name in ("first", "second", "by_token", "res")
-            )
-            pick(first[:], v, pos1_t, 0, c)
-            pick(second[:], v, pos2_t, 1, c)
+            pick(both[:, 0:G], v, pos1_t, 0, c)
+            pick(both[:, G : 2 * G], v, pos2_t, 1, c)
+            return both[:, 0:G], both[:, G : 2 * G]
+
+        blocks = [slice(j * P, (j + 1) * P) for j in range(2)]
+        there, back = gate_banks[0:2], gate_banks[2:4]
+        for u in range(5):
+            c, v = divmod(u, 2)
+            by_token, res = (keep.tile([P, G], F32, name="%s%d" % (name, u)) for name in ("by_token", "res"))
+            first, second = picked(u)
             for block in blocks:
-                turn_and_add(banks[sum_bank][:, block], (first[:, block], second[:, block]))
-            nc.scalar.copy(by_token[:], banks[sum_bank][:, 0:G])
+                turn_and_add(there[u % 2][:, block], (first[:, block], second[:, block]))
+            nc.scalar.copy(by_token[:], there[u % 2][:, 0:G])
             for j, block in enumerate(blocks):
-                turn_and_add(banks[back_bank][:, block], (shared[c][:, j, v * P : (v + 1) * P], by_token[:, block]))
-            nc.scalar.copy(res[:], banks[back_bank][:, 0:G])
+                turn_and_add(back[u % 2][:, block], (shared[c][:, j, v * P : (v + 1) * P], by_token[:, block]))
+            nc.scalar.copy(res[:], back[u % 2][:, 0:G])
             nc.sync.dma_start(out=out[v * P : (v + 1) * P, c * G : (c + 1) * G], in_=res[:])
 
-        c = 2
-        first, second, part, res = (
-            keep.tile([P, 2, G], F32, name="late_" + name) for name in ("first", "second", "part", "res")
-        )
-        for v in range(2):
-            pick(first[:, v, :], v, pos1_t, 0, c)
-        pick(second[:, 0, :], 0, pos2_t, 1, c)
-        nc.vector.tensor_tensor(
-            part[:].rearrange("p v t -> p (v t)"), last[:], first[:].rearrange("p v t -> p (v t)"), ADD
-        )
-        pick(second[:, 1, :], 1, pos2_t, 1, c)
-        for v in range(2):
-            nc.vector.tensor_tensor(res[:, v, :], part[:, v, :], second[:, v, :], ADD)
-            nc.sync.dma_start(out=out[v * P : (v + 1) * P, c * G : (c + 1) * G], in_=res[:, v, :])
+        part, res = (keep.tile([P, G], F32, name="late_" + name) for name in ("part", "res"))
+        first, second = picked(5)
+        nc.vector.tensor_tensor(part[:], last, first, ADD)
+        nc.vector.tensor_tensor(res[:], part[:], second, ADD)
+        nc.sync.dma_start(out=out[P:N, 2 * G : T], in_=res[:])

@@ -61,9 +61,9 @@ def tile_moe_shf_glu_gelu_kernel(
         gate_t = keep.tile([P, 2, T], F32, name="gate_t")
         ident = keep.tile([P, P], F32, name="ident")
 
-        for plane in (xs, s1s, s3s, s2s):
+        for plane in (xs,):
             nc.gpsimd.memset(plane[:].bitcast(I32), 0)
-        for plane in (s1, s3, s2):
+        for plane in (s1s, s3, s1, s2, s3s, s2s):
             nc.vector.memset(plane[:].bitcast(I32), 0)
         make_identity(nc, ident[:])
 
@@ -87,19 +87,18 @@ def tile_moe_shf_glu_gelu_kernel(
         load_scales(nc.scalar, (2, 1, 3), xs[:], x_scales)
         load_tokens(slice(T // 2, T))
         nc.sync.dma_start(offs_t[:], offs)
-        load_fp4(nc.sync, w1_words, w1, "w1", 0, 1)
-        load_scales(nc.scalar, (1, 3), s1[:], w1_scales[:, 0])
-        load_scales(nc.sync, (0, 2), s1[:], w1_scales[:, 0])
-        load_scales(nc.gpsimd, (1, 3), s3[:], w3_scales[:, 0])
-        load_fp4(nc.sync, w1_words, w1, "w1", 1, 4)
-        load_fp4(nc.sync, w1_words, w1, "w1", 4, 6)
-        load_fp4(nc.sync, w3_words, w3, "w3", 0, 2)
-        load_scales(nc.sync, (0, 2), s3[:], w3_scales[:, 0])
+        load_scales(nc.scalar, (1, 3), s1s[:], w1s_scales)
         load_fp8(nc.sync, w1s, w1s_words)
-        load_scales(nc.gpsimd, (1, 3), s2[:], w2_scales[:, 0])
-        load_scales(nc.gpsimd, ports, s1s[:], w1s_scales)
+        load_scales(nc.sync, (0, 2), s1s[:], w1s_scales)
+        load_scales(nc.scalar, (1, 3), s3[:], w3_scales[:, 0])
+        load_scales(nc.gpsimd, (1, 3), s1[:], w1_scales[:, 0])
+        load_scales(nc.sync, (0, 2), s3[:], w3_scales[:, 0])
+        load_fp4(nc.sync, w3_words, w3, "w3", 0, 2)
+        load_fp4(nc.sync, w1_words, w1, "w1", 0, 2)
+        load_scales(nc.sync, (0, 2), s1[:], w1_scales[:, 0])
+        load_fp4(nc.sync, w1_words, w1, "w1", 2, 6)
         load_fp4(nc.sync, w3_words, w3, "w3", 2, 4)
-        load_scales(nc.sync, (0, 2), s2[:], w2_scales[:, 0])
+        load_scales(nc.gpsimd, ports, s2[:], w2_scales[:, 0])
         load_fp4(nc.sync, w2_words, w2, "w2", 0, 6)
         load_fp4(nc.sync, w3_words, w3, "w3", 4, 6)
         load_fp8(nc.sync, w3s, w3s_words)
@@ -112,14 +111,13 @@ def tile_moe_shf_glu_gelu_kernel(
 
         y = [keep.tile([P, S], F32, name="y%d" % v) for v in range(2)]
         banks = [psum.tile([P, H], F32, name="bank%d" % k) for k in range(8)]
-        first_banks, turn_bank, sum_bank = banks[0:6], banks[6], banks[7]
         got_words, got_scales = {}, {}
         acts = tiles("act", 2 * GROUPS, [P, 2, P, 2], F32)
         hidden = tiles("h", 2 * GROUPS, [P, 2, P, 2], BF16)
         turned = tiles("ht", GROUPS, [P, 4 * G], BF16)
         codes = tiles("hq", GROUPS, [P, G], U32)
         code_scales = tiles("hs", GROUPS, [P, G], U8)
-        shared = tiles("shared", 3, [P, 2, N], F32)
+        shared = tiles("shared", 2, [P, 2, N], F32)
 
         def gather(e, count):
             for held, window, name in ((got_scales, xs[:, 0, :], "got_scales"), (got_words, xw[:].bitcast(U32), "got_words")):
@@ -151,14 +149,15 @@ def tile_moe_shf_glu_gelu_kernel(
             sums = first_product(bank, k, w3, s3, w3s, s3s)
             nc.vector.tensor_tensor(hidden[k][:], sums, acts[k][:], MULT)
 
-        def turn(g):
-            tr = turn_bank[:].rearrange("p (j u r) -> p j u r", j=2, u=2)
-            for j in range(2):
+        def turn(g, bank):
+            tr = bank[:].rearrange("p (j u r) -> p j u r", j=2, u=2)
+            for j in (1, 0):
                 pairs = hidden[2 * g + j][:].rearrange("p u m e -> p (u m e)").bitcast(F32)
                 for u in range(2):
                     nc.tensor.transpose(tr[:, j, u, :], pairs[:, u * P : (u + 1) * P], ident[:])
             ht = turned[g]
-            nc.scalar.copy(
+            copy = nc.vector.tensor_copy if False else nc.scalar.copy
+            copy(
                 ht[:].bitcast(F32).rearrange("p (j r u) -> p j r u", j=2, u=2), tr.rearrange("p j u r -> p j r u")
             )
 
@@ -171,50 +170,49 @@ def tile_moe_shf_glu_gelu_kernel(
                 start=True, stop=True,
             )
 
-        def second_routed(g):
+        def second_routed(g, sum_bank):
             for v in range(2):
                 cols = slice(v * P, (v + 1) * P)
                 by_feature(sum_bank[:, v * G : (v + 1) * G], g, w2[g][:, 2 * v * P : 2 * (v + 1) * P].bitcast(FP4X4), s2[:, g, cols])
             for v in range(2):
-                nc.scalar.copy(y[v][:, g * C : (g + 1) * C], sum_bank[:, v * G : (v + 1) * G])
+                copy = nc.vector.tensor_copy if g == E - 1 else nc.scalar.copy
+                copy(y[v][:, g * C : (g + 1) * C], sum_bank[:, v * G : (v + 1) * G])
 
-        def second_shared(c, width):
+        def second_shared(c, sum_bank):
             for j in range(2):
                 nc.tensor.matmul_mx(
-                    out=sum_bank[:, j * N : j * N + width],
+                    out=sum_bank[:, j * N : (j + 1) * N],
                     lhsT=codes[E + c][:, j * P : (j + 1) * P].bitcast(FP8X4),
                     lhsT_scale=code_scales[E + c][:, j * P : (j + 1) * P],
-                    rhs=w2s[:, 0:width].bitcast(FP8X4), rhs_scale=s2s[:, 0, 0:width], start=True, stop=True,
+                    rhs=w2s[:].bitcast(FP8X4), rhs_scale=s2s[:, 0, :], start=True, stop=True,
                 )
-            nc.scalar.copy(shared[c][:, :, 0:width], sum_bank[:].rearrange("p (j n) -> p j n", j=2)[:, :, 0:width])
+            nc.scalar.copy(shared[c][:].rearrange("p j n -> p (j n)"), sum_bank[:])
 
         for e in range(E):
             gather(e, 1)
-        gelu_banks, gate_banks = first_banks[0:3], first_banks[3:6] + first_banks[0:1]
-        last = gelu_banks[1][:, 0:G]
+        gelu_banks, gate_banks = banks[0:3], [banks[b] for b in (3,4,5,7)]
+        turn_banks, sum_banks, last = [banks[b] for b in (6,0)], [banks[b] for b in (1,2)], banks[7]
 
-        def behind(g):
-            if 0 <= g < GROUPS:
-                turn(g)
+        def second(g):
+            if g < E:
+                second_routed(g, sum_banks[g % len(sum_banks)])
+            elif g < GROUPS - 1:
+                second_shared(g - E, sum_banks[g % len(sum_banks)])
+
+        for k in list(range(2 * E, 2 * GROUPS)) + list(range(12)):
+            gelu_side(k, gelu_banks[k % len(gelu_banks)])
+        for k in range(2 * GROUPS + 3):
+            if k < 2 * GROUPS:
+                gate_side(k, gate_banks[k % len(gate_banks)])
+            g, odd = divmod(k - 3, 2)
+            if not odd and 0 <= g < GROUPS:
+                turn(g, turn_banks[g % len(turn_banks)])
                 quantise(g)
-            if 0 <= g - 1 < E:
-                second_routed(g - 1)
-            elif E <= g - 1 < GROUPS - 1:
-                second_shared(g - 1 - E, N)
-            elif g == GROUPS:
-                second_shared(g - 1 - E, P)
-                by_feature(last, g - 1, w2s[:, P:N].bitcast(FP8X4), s2s[:, 0, P:N])
-
-        for k in range(2 * E):
-            gelu_side(k, gelu_banks[k % 3])
-        for k in range(2 * GROUPS):
-            if 2 * E <= k + 2 < 2 * GROUPS:
-                gelu_side(k + 2, gelu_banks[1 + k % 2])
-            gate_side(k, gate_banks[k % 4])
-            if (k - 4) % 2 == 0:
-                behind((k - 4) // 2)
-        for g in range((2 * GROUPS - 4 + 1) // 2, GROUPS + 1):
-            behind(g)
+            g, odd = divmod(k - 3, 2)
+            if not odd and 0 <= g < GROUPS:
+                second(g)
+            if k + 12 < 2 * E:
+                gelu_side(k + 12, gelu_banks[(k + 12) % len(gelu_banks)])
 
         def pick(into, v, places, r, c):
             nc.vector.tensor_tensor(
@@ -226,28 +224,33 @@ def tile_moe_shf_glu_gelu_kernel(
                 nc.tensor.matmul(into, term, ident[:], start=(k == 0), stop=(k == len(terms) - 1), is_transpose=True)
 
         def picked(u):
-            both = acts[2 * GROUPS - 2 + u % 2][:].rearrange("p u m e -> p (u m e)")
+            both = keep.tile([P, 2 * G], F32, name="picked%d" % u)
             c, v = divmod(u, 2)
             pick(both[:, 0:G], v, pos1_t, 0, c)
             pick(both[:, G : 2 * G], v, pos2_t, 1, c)
             return both[:, 0:G], both[:, G : 2 * G]
 
         blocks = [slice(j * P, (j + 1) * P) for j in range(2)]
-        there, back = gate_banks[0:2], gate_banks[2:4]
-        for u in range(5):
+        there, back = [banks[b] for b in (3,4)], [banks[b] for b in (5,6)]
+        for u in range(4):
             c, v = divmod(u, 2)
-            by_token, res = (keep.tile([P, G], F32, name="%s%d" % (name, u)) for name in ("by_token", "res"))
+            part, res = (keep.tile([P, G], F32, name="%s%d" % (name, u)) for name in ("part", "res"))
             first, second = picked(u)
+            if u == 3:
+                for half, block in enumerate(blocks):
+                    by_feature(last[:, half * G : (half + 1) * G], GROUPS - 1, w2s[:, block].bitcast(FP8X4), s2s[:, 0, block])
             for block in blocks:
-                turn_and_add(there[u % 2][:, block], (first[:, block], second[:, block]))
-            nc.scalar.copy(by_token[:], there[u % 2][:, 0:G])
+                turn_and_add(there[u % 2][:, block], (second[:, block], first[:, block]))
+            nc.scalar.copy(part[:], there[u % 2][:, 0:G])
             for j, block in enumerate(blocks):
-                turn_and_add(back[u % 2][:, block], (shared[c][:, j, v * P : (v + 1) * P], by_token[:, block]))
+                turn_and_add(back[u % 2][:, block], (part[:, block], shared[c][:, j, v * P : (v + 1) * P]))
             nc.scalar.copy(res[:], back[u % 2][:, 0:G])
             nc.sync.dma_start(out=out[v * P : (v + 1) * P, c * G : (c + 1) * G], in_=res[:])
 
-        part, res = (keep.tile([P, G], F32, name="late_" + name) for name in ("part", "res"))
-        first, second = picked(5)
-        nc.vector.tensor_tensor(part[:], last, first, ADD)
-        nc.vector.tensor_tensor(res[:], part[:], second, ADD)
-        nc.sync.dma_start(out=out[P:N, 2 * G : T], in_=res[:])
+        late = [picked(4 + v) for v in range(2)]
+        parts, results = tiles("late_part", 2, [P, G], F32), tiles("late_res", 2, [P, G], F32)
+        for v in range(2):
+            nc.vector.tensor_tensor(parts[v][:], last[:, v * G : (v + 1) * G], late[v][0], ADD)
+        for v in range(2):
+            nc.vector.tensor_tensor(results[v][:], parts[v][:], late[v][1], ADD)
+            nc.sync.dma_start(out=out[v * P : (v + 1) * P, 2 * G : T], in_=results[v][:])

@@ -61,11 +61,10 @@ def tile_moe_shf_glu_gelu_kernel(
         gate_t = keep.tile([P, 2, T], F32, name="gate_t")
         ident = keep.tile([P, P], F32, name="ident")
 
-        for plane in (xs,):
+        for plane in (s2,):
             nc.gpsimd.memset(plane[:].bitcast(I32), 0)
-        for plane in (s1s, s3, s1, s2, s3s, s2s):
+        for plane in (xs, s1s, s3, s1, s3s, s2s):
             nc.vector.memset(plane[:].bitcast(I32), 0)
-        make_identity(nc, ident[:])
 
         w1, w3, w2 = {}, {}, {}
 
@@ -79,35 +78,30 @@ def tile_moe_shf_glu_gelu_kernel(
             queue.dma_start(out=t[:], in_=words[0].rearrange("p n d -> p (n d)").bitcast(I32))
 
         ports = (0, 2, 1, 3)
-        def load_tokens(half):
-            nc.sync.dma_start(out=xw[:, half], in_=x_words[0, :, half].rearrange("p n d -> p (n d)").bitcast(I32))
-
-        load_tokens(slice(0, T // 2))
+        nc.sync.dma_start(offs_t[:], offs)
         load_scales(nc.sync, (0,), xs[:], x_scales)
         load_scales(nc.scalar, (2, 1, 3), xs[:], x_scales)
-        load_tokens(slice(T // 2, T))
-        nc.sync.dma_start(offs_t[:], offs)
-        load_scales(nc.scalar, (1, 3), s1s[:], w1s_scales)
+        load_fp8(nc.sync, xw, x_words)
         load_fp8(nc.sync, w1s, w1s_words)
+        load_scales(nc.scalar, (1, 3), s1s[:], w1s_scales)
         load_scales(nc.sync, (0, 2), s1s[:], w1s_scales)
-        load_scales(nc.scalar, (1, 3), s3[:], w3_scales[:, 0])
-        load_scales(nc.gpsimd, (1, 3), s1[:], w1_scales[:, 0])
-        load_scales(nc.sync, (0, 2), s3[:], w3_scales[:, 0])
+        load_scales(nc.gpsimd, ports, s2[:], w2_scales[:, 0])
+        make_identity(nc, ident[:])
+        load_scales(nc.sync, ports, s3[:], w3_scales[:, 0])
         load_fp4(nc.sync, w3_words, w3, "w3", 0, 2)
         load_fp4(nc.sync, w1_words, w1, "w1", 0, 2)
-        load_scales(nc.sync, (0, 2), s1[:], w1_scales[:, 0])
+        load_scales(nc.sync, ports, s1[:], w1_scales[:, 0])
         load_fp4(nc.sync, w1_words, w1, "w1", 2, 6)
         load_fp4(nc.sync, w3_words, w3, "w3", 2, 4)
-        load_scales(nc.gpsimd, ports, s2[:], w2_scales[:, 0])
-        load_fp4(nc.sync, w2_words, w2, "w2", 0, 6)
         load_fp4(nc.sync, w3_words, w3, "w3", 4, 6)
+        load_fp4(nc.sync, w2_words, w2, "w2", 0, 6)
         load_fp8(nc.sync, w3s, w3s_words)
         load_scales(nc.sync, ports, s3s[:], w3s_scales)
-        load_scales(nc.gpsimd, ports, s2s[:], w2s_scales)
         load_fp8(nc.sync, w2s, w2s_words)
         nc.sync.dma_start(pos1_t[:], pos1)
         nc.sync.dma_start(pos2_t[:], pos2)
         nc.sync.dma_start(out=gate_t[:], in_=gate.rearrange("r p t -> p r t"))
+        load_scales(nc.sync, ports, s2s[:], w2s_scales)
 
         y = [keep.tile([P, S], F32, name="y%d" % v) for v in range(2)]
         banks = [psum.tile([P, H], F32, name="bank%d" % k) for k in range(8)]
@@ -119,12 +113,11 @@ def tile_moe_shf_glu_gelu_kernel(
         code_scales = tiles("hs", GROUPS, [P, G], U8)
         shared = tiles("shared", 2, [P, 2, N], F32)
 
-        def gather(e, count):
-            for held, window, name in ((got_scales, xs[:, 0, :], "got_scales"), (got_words, xw[:].bitcast(U32), "got_words")):
-                into = keep.tile([P, count * C], window.dtype, name="%s%d" % (name, e), align_bytes=64)
-                nc.vector.tensor_copy(into[:], window.indirect(offs_t[:, e * C // 16 : (e + count) * C // 16]))
-                for i in range(count):
-                    held[e + i] = into[:, i * C : (i + 1) * C]
+        def gather(held, window, name, e, count):
+            into = keep.tile([P, count * C], window.dtype, name="%s%d" % (name, e), align_bytes=64)
+            nc.vector.tensor_copy(into[:], window.indirect(offs_t[:, e * C // 16 : (e + count) * C // 16]))
+            for i in range(count):
+                held[e + i] = into[:, i * C : (i + 1) * C]
 
         def first_product(acc, k, routed, routed_scales, common, common_scales):
             g, j = divmod(k, 2)
@@ -156,8 +149,7 @@ def tile_moe_shf_glu_gelu_kernel(
                 for u in range(2):
                     nc.tensor.transpose(tr[:, j, u, :], pairs[:, u * P : (u + 1) * P], ident[:])
             ht = turned[g]
-            copy = nc.vector.tensor_copy if False else nc.scalar.copy
-            copy(
+            nc.scalar.copy(
                 ht[:].bitcast(F32).rearrange("p (j r u) -> p j r u", j=2, u=2), tr.rearrange("p j u r -> p j r u")
             )
 
@@ -175,8 +167,7 @@ def tile_moe_shf_glu_gelu_kernel(
                 cols = slice(v * P, (v + 1) * P)
                 by_feature(sum_bank[:, v * G : (v + 1) * G], g, w2[g][:, 2 * v * P : 2 * (v + 1) * P].bitcast(FP4X4), s2[:, g, cols])
             for v in range(2):
-                copy = nc.vector.tensor_copy if g == E - 1 else nc.scalar.copy
-                copy(y[v][:, g * C : (g + 1) * C], sum_bank[:, v * G : (v + 1) * G])
+                nc.scalar.copy(y[v][:, g * C : (g + 1) * C], sum_bank[:, v * G : (v + 1) * G])
 
         def second_shared(c, sum_bank):
             for j in range(2):
@@ -188,8 +179,9 @@ def tile_moe_shf_glu_gelu_kernel(
                 )
             nc.scalar.copy(shared[c][:].rearrange("p j n -> p (j n)"), sum_bank[:])
 
-        for e in range(E):
-            gather(e, 1)
+        for e in range(0, E, 2):
+            gather(got_scales, xs[:, 0, :], "got_scales", e, 2)
+            gather(got_words, xw[:].bitcast(U32), "got_words", e, 2)
         gelu_banks, gate_banks = banks[0:3], [banks[b] for b in (3,4,5,7)]
         turn_banks, sum_banks, last = [banks[b] for b in (6,0)], [banks[b] for b in (1,2)], banks[7]
 

@@ -183,12 +183,12 @@ def tile_moe_shf_glu_gelu_kernel(
             gather(got_scales, xs[:, 0, :], "got_scales", e, 2)
             gather(got_words, xw[:].bitcast(U32), "got_words", e, 2)
         gelu_banks, gate_banks = banks[0:3], [banks[b] for b in (3,4,5,7)]
-        turn_banks, sum_banks, last = [banks[b] for b in (6,0)], [banks[b] for b in (1,2)], banks[7]
+        turn_banks, sum_banks = [banks[b] for b in (6,0)], [banks[b] for b in (1,2)]
 
         def second(g):
             if g < E:
                 second_routed(g, sum_banks[g % len(sum_banks)])
-            elif g < GROUPS - 1:
+            elif g == E:
                 second_shared(g - E, sum_banks[g % len(sum_banks)])
 
         for k in list(range(2 * E, 2 * GROUPS)) + list(range(12)):
@@ -224,16 +224,19 @@ def tile_moe_shf_glu_gelu_kernel(
 
         blocks = [slice(j * P, (j + 1) * P) for j in range(2)]
         there, back = [banks[b] for b in (3,4)], [banks[b] for b in (5,6)]
+        last = there[0]
         for u in range(4):
             c, v = divmod(u, 2)
             part, res = (keep.tile([P, G], F32, name="%s%d" % (name, u)) for name in ("part", "res"))
             first, second = picked(u)
-            if u == 3:
-                for half, block in enumerate(blocks):
-                    by_feature(last[:, half * G : (half + 1) * G], GROUPS - 1, w2s[:, block].bitcast(FP8X4), s2s[:, 0, block])
             for block in blocks:
                 turn_and_add(there[u % 2][:, block], (second[:, block], first[:, block]))
             nc.scalar.copy(part[:], there[u % 2][:, 0:G])
+            if u == 0:
+                second_shared(1, there[0])
+            if u == 2:
+                for half, block in enumerate(blocks):
+                    by_feature(last[:, half * G : (half + 1) * G], GROUPS - 1, w2s[:, block].bitcast(FP8X4), s2s[:, 0, block])
             for j, block in enumerate(blocks):
                 turn_and_add(back[u % 2][:, block], (part[:, block], shared[c][:, j, v * P : (v + 1) * P]))
             nc.scalar.copy(res[:], back[u % 2][:, 0:G])

@@ -111,7 +111,7 @@ def tile_moe_shf_glu_gelu_kernel(
         turned = tiles("ht", GROUPS, [P, 4 * G], BF16)
         codes = tiles("hq", GROUPS, [P, G], U32)
         code_scales = tiles("hs", GROUPS, [P, G], U8)
-        shared = tiles("shared", 2, [P, 2, N], F32)
+        shared = [keep.tile([P, 2 * width], F32, name="shared%d" % c) for c, width in enumerate((N, P, P))]
 
         def gather(held, window, name, e, count):
             into = keep.tile([P, count * C], window.dtype, name="%s%d" % (name, e), align_bytes=64)
@@ -162,22 +162,22 @@ def tile_moe_shf_glu_gelu_kernel(
                 start=True, stop=True,
             )
 
-        def second_routed(g, sum_bank):
-            for v in range(2):
-                cols = slice(v * P, (v + 1) * P)
-                by_feature(sum_bank[:, v * G : (v + 1) * G], g, w2[g][:, 2 * v * P : 2 * (v + 1) * P].bitcast(FP4X4), s2[:, g, cols])
-            for v in range(2):
-                nc.scalar.copy(y[v][:, g * C : (g + 1) * C], sum_bank[:, v * G : (v + 1) * G])
+        def second_routed(v, experts, bank):
+            cols = slice(v * P, (v + 1) * P)
+            for i, g in enumerate(experts):
+                w = w2[g][:, 2 * v * P : 2 * (v + 1) * P].bitcast(FP4X4)
+                by_feature(bank[:, i * G : (i + 1) * G], g, w, s2[:, g, cols])
+            nc.scalar.copy(y[v][:, experts[0] * C : (experts[-1] + 1) * C], bank[:, 0 : len(experts) * G])
 
-        def second_shared(c, sum_bank):
+        def second_shared(c, bank, width):
             for j in range(2):
                 nc.tensor.matmul_mx(
-                    out=sum_bank[:, j * N : (j + 1) * N],
+                    out=bank[:, j * width : (j + 1) * width],
                     lhsT=codes[E + c][:, j * P : (j + 1) * P].bitcast(FP8X4),
                     lhsT_scale=code_scales[E + c][:, j * P : (j + 1) * P],
-                    rhs=w2s[:].bitcast(FP8X4), rhs_scale=s2s[:, 0, :], start=True, stop=True,
+                    rhs=w2s[:, 0:width].bitcast(FP8X4), rhs_scale=s2s[:, 0, 0:width], start=True, stop=True,
                 )
-            nc.scalar.copy(shared[c][:].rearrange("p j n -> p (j n)"), sum_bank[:])
+            nc.scalar.copy(shared[c][:], bank[:, 0 : 2 * width])
 
         for e in range(0, E, 2):
             gather(got_scales, xs[:, 0, :], "got_scales", e, 2)
@@ -187,9 +187,9 @@ def tile_moe_shf_glu_gelu_kernel(
 
         def second(g):
             if g < E:
-                second_routed(g, sum_banks[g % len(sum_banks)])
-            elif g == E:
-                second_shared(g - E, sum_banks[g % len(sum_banks)])
+                second_routed(0, [g], sum_banks[g % len(sum_banks)])
+            elif g < GROUPS - 1:
+                second_shared(g - E, sum_banks[g % len(sum_banks)], N if g == E else P)
 
         for k in list(range(2 * E, 2 * GROUPS)) + list(range(12)):
             gelu_side(k, gelu_banks[k % len(gelu_banks)])
@@ -203,49 +203,48 @@ def tile_moe_shf_glu_gelu_kernel(
             g, odd = divmod(k - 3, 2)
             if not odd and 0 <= g < GROUPS:
                 second(g)
+            if k == 19:
+                for e, b in zip(range(0, E, 2), (5, 7, 3)):
+                    second_routed(1, [e, e + 1], banks[b])
             if k + 12 < 2 * E:
                 gelu_side(k + 12, gelu_banks[(k + 12) % len(gelu_banks)])
 
-        def pick(into, v, places, r, c):
-            nc.vector.tensor_tensor(
-                into, y[v][:].indirect(places[:, c * G // 16 : (c + 1) * G // 16]), gate_t[:, r, c * G : (c + 1) * G], MULT
-            )
+        def pick(into, v, places, r, tokens):
+            window = y[v][:].indirect(places[:, tokens.start // 16 : tokens.stop // 16])
+            nc.vector.tensor_tensor(into, window, gate_t[:, r, tokens], MULT)
 
         def turn_and_add(into, terms):
             for k, term in enumerate(terms):
                 nc.tensor.matmul(into, term, ident[:], start=(k == 0), stop=(k == len(terms) - 1), is_transpose=True)
 
-        def picked(u):
-            both = keep.tile([P, 2 * G], F32, name="picked%d" % u)
-            c, v = divmod(u, 2)
-            pick(both[:, 0:G], v, pos1_t, 0, c)
-            pick(both[:, G : 2 * G], v, pos2_t, 1, c)
-            return both[:, 0:G], both[:, G : 2 * G]
-
         blocks = [slice(j * P, (j + 1) * P) for j in range(2)]
-        there, back = [banks[b] for b in (3,4)], [banks[b] for b in (5,6)]
-        last = there[0]
-        for u in range(4):
-            c, v = divmod(u, 2)
-            part, res = (keep.tile([P, G], F32, name="%s%d" % (name, u)) for name in ("part", "res"))
-            first, second = picked(u)
+        there, back = [banks[b] for b in (4, 0, 4, 0)], [banks[b] for b in (1, 2, 3, 6)]
+        last = back[1]
+        for u, (c, v) in enumerate(((0, 0), (1, 0), (2, 0), (0, 1))):
+            first, second, part, res = tiles("unit%d_" % u, 4, [P, G], F32)
+            tokens = slice(c * G, (c + 1) * G)
+            pick(first[:], v, pos1_t, 0, tokens)
+            pick(second[:], v, pos2_t, 1, tokens)
             for block in blocks:
-                turn_and_add(there[u % 2][:, block], (second[:, block], first[:, block]))
-            nc.scalar.copy(part[:], there[u % 2][:, 0:G])
-            if u == 0:
-                second_shared(1, there[0])
+                turn_and_add(there[u][:, block], (second[:, block], first[:, block]))
+            nc.scalar.copy(part[:], there[u][:, 0:G])
             if u == 2:
-                for half, block in enumerate(blocks):
-                    by_feature(last[:, half * G : (half + 1) * G], GROUPS - 1, w2s[:, block].bitcast(FP8X4), s2s[:, 0, block])
+                second_shared(2, back[0], P)
+            if u == 3:
+                for i in range(2):
+                    by_feature(last[:, i * G : (i + 1) * G], E + 1 + i, w2s[:, P:N].bitcast(FP8X4), s2s[:, 0, P:N])
+            sums = shared[c][:].rearrange("p (j n) -> p j n", j=2)
             for j, block in enumerate(blocks):
-                turn_and_add(back[u % 2][:, block], (part[:, block], shared[c][:, j, v * P : (v + 1) * P]))
-            nc.scalar.copy(res[:], back[u % 2][:, 0:G])
-            nc.sync.dma_start(out=out[v * P : (v + 1) * P, c * G : (c + 1) * G], in_=res[:])
+                turn_and_add(back[u][:, block], (part[:, block], sums[:, j, v * P : (v + 1) * P]))
+            nc.scalar.copy(res[:], back[u][:, 0:G])
+            nc.sync.dma_start(out=out[v * P : (v + 1) * P, tokens], in_=res[:])
 
-        late = [picked(4 + v) for v in range(2)]
-        parts, results = tiles("late_part", 2, [P, G], F32), tiles("late_res", 2, [P, G], F32)
-        for v in range(2):
-            nc.vector.tensor_tensor(parts[v][:], last[:, v * G : (v + 1) * G], late[v][0], ADD)
-        for v in range(2):
-            nc.vector.tensor_tensor(results[v][:], parts[v][:], late[v][1], ADD)
-            nc.sync.dma_start(out=out[v * P : (v + 1) * P, 2 * G : T], in_=results[v][:])
+        first, second, part, res = tiles("late", 4, [P, T - G], F32)
+        pick(first[:], 1, pos1_t, 0, slice(G, T))
+        pick(second[:], 1, pos2_t, 1, slice(G, T))
+        halves = [slice(i * G, (i + 1) * G) for i in range(2)]
+        for half in halves:
+            nc.vector.tensor_tensor(part[:, half], last[:, half], first[:, half], ADD)
+        for i, half in enumerate(halves):
+            nc.vector.tensor_tensor(res[:, half], part[:, half], second[:, half], ADD)
+            nc.sync.dma_start(out=out[P:N, (i + 1) * G : (i + 2) * G], in_=res[:, half])

@@ -111,7 +111,7 @@ def tile_moe_shf_glu_gelu_kernel(
         turned = tiles("ht", GROUPS, [P, 4 * G], BF16)
         codes = tiles("hq", GROUPS, [P, G], U32)
         code_scales = tiles("hs", GROUPS, [P, G], U8)
-        shared = [keep.tile([P, 2 * width], F32, name="shared%d" % c) for c, width in enumerate((N, P, P))]
+        shared = tiles("shared", GROUPS - E, [P, G], F32)
 
         def gather(held, window, name, e, count):
             into = keep.tile([P, count * C], window.dtype, name="%s%d" % (name, e), align_bytes=64)
@@ -169,15 +169,15 @@ def tile_moe_shf_glu_gelu_kernel(
                 by_feature(bank[:, i * G : (i + 1) * G], g, w, s2[:, g, cols])
             nc.scalar.copy(y[v][:, experts[0] * C : (experts[-1] + 1) * C], bank[:, 0 : len(experts) * G])
 
-        def second_shared(c, bank, width):
+        def second_shared(c, bank):
             for j in range(2):
                 nc.tensor.matmul_mx(
-                    out=bank[:, j * width : (j + 1) * width],
+                    out=bank[:, j * P : (j + 1) * P],
                     lhsT=codes[E + c][:, j * P : (j + 1) * P].bitcast(FP8X4),
                     lhsT_scale=code_scales[E + c][:, j * P : (j + 1) * P],
-                    rhs=w2s[:, 0:width].bitcast(FP8X4), rhs_scale=s2s[:, 0, 0:width], start=True, stop=True,
+                    rhs=w2s[:, 0:P].bitcast(FP8X4), rhs_scale=s2s[:, 0, 0:P], start=True, stop=True,
                 )
-            nc.scalar.copy(shared[c][:], bank[:, 0 : 2 * width])
+            nc.scalar.copy(shared[c][:], bank[:, 0:G])
 
         for e in range(0, E, 2):
             gather(got_scales, xs[:, 0, :], "got_scales", e, 2)
@@ -189,7 +189,7 @@ def tile_moe_shf_glu_gelu_kernel(
             if g < E:
                 second_routed(0, [g], sum_banks[g % len(sum_banks)])
             elif g < GROUPS - 1:
-                second_shared(g - E, sum_banks[g % len(sum_banks)], N if g == E else P)
+                second_shared(g - E, sum_banks[g % len(sum_banks)])
 
         for k in list(range(2 * E, 2 * GROUPS)) + list(range(12)):
             gelu_side(k, gelu_banks[k % len(gelu_banks)])
@@ -218,33 +218,34 @@ def tile_moe_shf_glu_gelu_kernel(
                 nc.tensor.matmul(into, term, ident[:], start=(k == 0), stop=(k == len(terms) - 1), is_transpose=True)
 
         blocks = [slice(j * P, (j + 1) * P) for j in range(2)]
-        there, back = [banks[b] for b in (4, 0, 4, 0)], [banks[b] for b in (1, 2, 3, 6)]
-        last = back[1]
-        for u, (c, v) in enumerate(((0, 0), (1, 0), (2, 0), (0, 1))):
-            first, second, part, res = tiles("unit%d_" % u, 4, [P, G], F32)
+        there, back = [banks[b] for b in (4, 0, 4)], [banks[b] for b in (1, 2, 3)]
+        upper = [banks[b][:, 0:G] for b in (6, 5, 2)]
+        for c in range(GROUPS - E):
+            first, second, part, res = tiles("unit%d_" % c, 4, [P, G], F32)
             tokens = slice(c * G, (c + 1) * G)
-            pick(first[:], v, pos1_t, 0, tokens)
-            pick(second[:], v, pos2_t, 1, tokens)
+            pick(first[:], 0, pos1_t, 0, tokens)
+            pick(second[:], 0, pos2_t, 1, tokens)
             for block in blocks:
-                turn_and_add(there[u][:, block], (second[:, block], first[:, block]))
-            nc.scalar.copy(part[:], there[u][:, 0:G])
-            if u == 2:
-                second_shared(2, back[0], P)
-            if u == 3:
-                for i in range(2):
-                    by_feature(last[:, i * G : (i + 1) * G], E + 1 + i, w2s[:, P:N].bitcast(FP8X4), s2s[:, 0, P:N])
-            sums = shared[c][:].rearrange("p (j n) -> p j n", j=2)
-            for j, block in enumerate(blocks):
-                turn_and_add(back[u][:, block], (part[:, block], sums[:, j, v * P : (v + 1) * P]))
-            nc.scalar.copy(res[:], back[u][:, 0:G])
-            nc.sync.dma_start(out=out[v * P : (v + 1) * P, tokens], in_=res[:])
+                turn_and_add(there[c][:, block], (second[:, block], first[:, block]))
+            nc.scalar.copy(part[:], there[c][:, 0:G])
+            if c == GROUPS - E - 1:
+                second_shared(c, back[0])
+            for block in blocks:
+                turn_and_add(back[c][:, block], (part[:, block], shared[c][:, block]))
+            nc.scalar.copy(res[:], back[c][:, 0:G])
+            nc.sync.dma_start(out=out[0:P, tokens], in_=res[:])
 
-        first, second, part, res = tiles("late", 4, [P, T - G], F32)
-        pick(first[:], 1, pos1_t, 0, slice(G, T))
-        pick(second[:], 1, pos2_t, 1, slice(G, T))
-        halves = [slice(i * G, (i + 1) * G) for i in range(2)]
-        for half in halves:
-            nc.vector.tensor_tensor(part[:, half], last[:, half], first[:, half], ADD)
-        for i, half in enumerate(halves):
-            nc.vector.tensor_tensor(res[:, half], part[:, half], second[:, half], ADD)
-            nc.sync.dma_start(out=out[P:N, (i + 1) * G : (i + 2) * G], in_=res[:, half])
+        for c in range(GROUPS - E):
+            by_feature(upper[c], E + c, w2s[:, P:N].bitcast(FP8X4), s2s[:, 0, P:N])
+        first, second, part, res = tiles("late", 4, [P, T], F32)
+        for tokens in (slice(0, G), slice(G, T)):
+            pick(first[:, tokens], 1, pos1_t, 0, tokens)
+            pick(second[:, tokens], 1, pos2_t, 1, tokens)
+            thirds = range(tokens.start // G, tokens.stop // G)
+            for c in thirds:
+                third = slice(c * G, (c + 1) * G)
+                nc.vector.tensor_tensor(part[:, third], upper[c], first[:, third], ADD)
+            for c in thirds:
+                third = slice(c * G, (c + 1) * G)
+                nc.vector.tensor_tensor(res[:, third], part[:, third], second[:, third], ADD)
+                nc.sync.dma_start(out=out[P:N, third], in_=res[:, third])

@@ -61,9 +61,9 @@ def tile_moe_shf_glu_gelu_kernel(
         gate_t = keep.tile([P, 2, T], F32, name="gate_t")
         ident = keep.tile([P, P], F32, name="ident")
 
-        for plane in (s2,):
+        for plane in (s2, s3, s3s, s2s):
             nc.gpsimd.memset(plane[:].bitcast(I32), 0)
-        for plane in (xs, s1s, s3, s1, s3s, s2s):
+        for plane in (xs, s1s, s1):
             nc.vector.memset(plane[:].bitcast(I32), 0)
 
         w1, w3, w2 = {}, {}, {}
@@ -79,39 +79,45 @@ def tile_moe_shf_glu_gelu_kernel(
 
         ports = (0, 2, 1, 3)
         nc.sync.dma_start(offs_t[:], offs)
-        load_scales(nc.sync, (0,), xs[:], x_scales)
-        load_scales(nc.scalar, (2, 1, 3), xs[:], x_scales)
+        nc.sync.dma_start(pos1_t[:], pos1)
+        load_scales(nc.sync, (0, 2), xs[:], x_scales)
+        load_scales(nc.scalar, (1, 3), xs[:], x_scales)
         load_fp8(nc.sync, xw, x_words)
         load_fp8(nc.sync, w1s, w1s_words)
-        load_scales(nc.scalar, (1, 3), s1s[:], w1s_scales)
-        load_scales(nc.sync, (0, 2), s1s[:], w1s_scales)
+        load_scales(nc.scalar, (0,), s1s[:], w1s_scales)
+        load_scales(nc.sync, (2, 1, 3), s1s[:], w1s_scales)
         load_scales(nc.gpsimd, ports, s2[:], w2_scales[:, 0])
         make_identity(nc, ident[:])
+        load_scales(nc.sync, ports, s1[:], w1_scales[:, 0])
+        load_fp4(nc.sync, w1_words, w1, "w1", 0, 2)
         load_scales(nc.sync, ports, s3[:], w3_scales[:, 0])
         load_fp4(nc.sync, w3_words, w3, "w3", 0, 2)
-        load_fp4(nc.sync, w1_words, w1, "w1", 0, 2)
-        load_scales(nc.sync, ports, s1[:], w1_scales[:, 0])
-        load_fp4(nc.sync, w1_words, w1, "w1", 2, 6)
+        load_fp4(nc.sync, w1_words, w1, "w1", 2, 4)
+        load_fp4(nc.sync, w1_words, w1, "w1", 4, 6)
         load_fp4(nc.sync, w3_words, w3, "w3", 2, 4)
         load_fp4(nc.sync, w3_words, w3, "w3", 4, 6)
         load_fp4(nc.sync, w2_words, w2, "w2", 0, 6)
         load_fp8(nc.sync, w3s, w3s_words)
         load_scales(nc.sync, ports, s3s[:], w3s_scales)
         load_fp8(nc.sync, w2s, w2s_words)
-        nc.sync.dma_start(pos1_t[:], pos1)
+        load_scales(nc.sync, ports, s2s[:], w2s_scales)
         nc.sync.dma_start(pos2_t[:], pos2)
         nc.sync.dma_start(out=gate_t[:], in_=gate.rearrange("r p t -> p r t"))
-        load_scales(nc.sync, ports, s2s[:], w2s_scales)
 
         y = [keep.tile([P, S], F32, name="y%d" % v) for v in range(2)]
         banks = [psum.tile([P, H], F32, name="bank%d" % k) for k in range(8)]
-        got_words, got_scales = {}, {}
+        scalar_ring = banks[0:4]
+        vector_ring = banks[4:8]
+        got_words, got_scales, gate_sums = {}, {}, {}
         acts = tiles("act", 2 * GROUPS, [P, 2, P, 2], F32)
         hidden = tiles("h", 2 * GROUPS, [P, 2, P, 2], BF16)
         turned = tiles("ht", GROUPS, [P, 4 * G], BF16)
         codes = tiles("hq", GROUPS, [P, G], U32)
         code_scales = tiles("hs", GROUPS, [P, G], U8)
-        shared = tiles("shared", GROUPS - E, [P, G], F32)
+
+        def take(ring):
+            ring[:] = ring[1:] + ring[:1]
+            return ring[-1]
 
         def gather(held, window, name, e, count):
             into = keep.tile([P, count * C], window.dtype, name="%s%d" % (name, e), align_bytes=64)
@@ -134,24 +140,30 @@ def tile_moe_shf_glu_gelu_kernel(
             )
             return acc[:].rearrange("p (m u e) -> p u m e", u=2, e=2)
 
-        def gelu_side(k, bank):
-            sums = first_product(bank, k, w1, s1, w1s, s1s)
+        def gelu_side(k):
+            sums = first_product(take(scalar_ring), k, w1, s1, w1s, s1s)
             nc.scalar.activation(acts[k][:], sums, GELU)
 
-        def gate_side(k, bank):
-            sums = first_product(bank, k, w3, s3, w3s, s3s)
-            nc.vector.tensor_tensor(hidden[k][:], sums, acts[k][:], MULT)
+        def gate_product(k):
+            if k < 2 * GROUPS:
+                gate_sums[k] = first_product(take(vector_ring), k, w3, s3, w3s, s3s)
 
-        def turn(g, bank):
-            tr = bank[:].rearrange("p (j u r) -> p j u r", j=2, u=2)
-            for j in (1, 0):
-                pairs = hidden[2 * g + j][:].rearrange("p u m e -> p (u m e)").bitcast(F32)
-                for u in range(2):
-                    nc.tensor.transpose(tr[:, j, u, :], pairs[:, u * P : (u + 1) * P], ident[:])
-            ht = turned[g]
-            nc.scalar.copy(
-                ht[:].bitcast(F32).rearrange("p (j r u) -> p j r u", j=2, u=2), tr.rearrange("p j u r -> p j r u")
-            )
+        def multiply(k):
+            nc.vector.tensor_tensor(hidden[k][:], gate_sums[k], acts[k][:], MULT)
+            gate_product(k + 4)
+
+        def turn(groups):
+            views = [take(scalar_ring)[:].rearrange("p (j u r) -> p j u r", j=2, u=2) for g in groups]
+            for g, tr in reversed(list(zip(groups, views))):
+                for j in (1, 0):
+                    pairs = hidden[2 * g + j][:].rearrange("p u m e -> p (u m e)").bitcast(F32)
+                    for u in range(2):
+                        nc.tensor.transpose(tr[:, j, u, :], pairs[:, u * P : (u + 1) * P], ident[:])
+            for g, tr in zip(groups, views):
+                nc.scalar.copy(
+                    turned[g][:].bitcast(F32).rearrange("p (j r u) -> p j r u", j=2, u=2),
+                    tr.rearrange("p j u r -> p j r u"),
+                )
 
         def quantise(g):
             nc.vector.quantize_mx(out=codes[g][:].bitcast(FP8X4), scales=code_scales[g][:], in_=turned[g][:])
@@ -162,52 +174,28 @@ def tile_moe_shf_glu_gelu_kernel(
                 start=True, stop=True,
             )
 
-        def second_routed(v, experts, bank):
+        def second_routed(v, experts, ring):
+            bank = take(ring)
             cols = slice(v * P, (v + 1) * P)
-            for i, g in enumerate(experts):
+            for g in experts:
                 w = w2[g][:, 2 * v * P : 2 * (v + 1) * P].bitcast(FP4X4)
+                i = g - min(experts)
                 by_feature(bank[:, i * G : (i + 1) * G], g, w, s2[:, g, cols])
-            nc.scalar.copy(y[v][:, experts[0] * C : (experts[-1] + 1) * C], bank[:, 0 : len(experts) * G])
+            nc.scalar.copy(y[v][:, min(experts) * C : (max(experts) + 1) * C], bank[:, 0 : len(experts) * G])
 
-        def second_shared(c, bank):
+        shared = {}
+
+        def second_shared(c, width):
+            bank = take(scalar_ring)
             for j in range(2):
                 nc.tensor.matmul_mx(
-                    out=bank[:, j * P : (j + 1) * P],
+                    out=bank[:, j * width : (j + 1) * width],
                     lhsT=codes[E + c][:, j * P : (j + 1) * P].bitcast(FP8X4),
                     lhsT_scale=code_scales[E + c][:, j * P : (j + 1) * P],
-                    rhs=w2s[:, 0:P].bitcast(FP8X4), rhs_scale=s2s[:, 0, 0:P], start=True, stop=True,
+                    rhs=w2s[:, 0:width].bitcast(FP8X4), rhs_scale=s2s[:, 0, 0:width], start=True, stop=True,
                 )
-            nc.scalar.copy(shared[c][:], bank[:, 0:G])
-
-        for e in range(0, E, 2):
-            gather(got_scales, xs[:, 0, :], "got_scales", e, 2)
-            gather(got_words, xw[:].bitcast(U32), "got_words", e, 2)
-        gelu_banks, gate_banks = banks[0:3], [banks[b] for b in (3,4,5,7)]
-        turn_banks, sum_banks = [banks[b] for b in (6,0)], [banks[b] for b in (1,2)]
-
-        def second(g):
-            if g < E:
-                second_routed(0, [g], sum_banks[g % len(sum_banks)])
-            elif g < GROUPS - 1:
-                second_shared(g - E, sum_banks[g % len(sum_banks)])
-
-        for k in list(range(2 * E, 2 * GROUPS)) + list(range(12)):
-            gelu_side(k, gelu_banks[k % len(gelu_banks)])
-        for k in range(2 * GROUPS + 3):
-            if k < 2 * GROUPS:
-                gate_side(k, gate_banks[k % len(gate_banks)])
-            g, odd = divmod(k - 3, 2)
-            if not odd and 0 <= g < GROUPS:
-                turn(g, turn_banks[g % len(turn_banks)])
-                quantise(g)
-            g, odd = divmod(k - 3, 2)
-            if not odd and 0 <= g < GROUPS:
-                second(g)
-            if k == 19:
-                for e, b in zip(range(0, E, 2), (5, 7, 3)):
-                    second_routed(1, [e, e + 1], banks[b])
-            if k + 12 < 2 * E:
-                gelu_side(k + 12, gelu_banks[(k + 12) % len(gelu_banks)])
+            shared[c] = keep.tile([P, 2, width], F32, name="shared%d" % c)
+            nc.scalar.copy(shared[c][:].rearrange("p j w -> p (j w)"), bank[:, 0 : 2 * width])
 
         def pick(into, v, places, r, tokens):
             window = y[v][:].indirect(places[:, tokens.start // 16 : tokens.stop // 16])
@@ -218,34 +206,94 @@ def tile_moe_shf_glu_gelu_kernel(
                 nc.tensor.matmul(into, term, ident[:], start=(k == 0), stop=(k == len(terms) - 1), is_transpose=True)
 
         blocks = [slice(j * P, (j + 1) * P) for j in range(2)]
-        there, back = [banks[b] for b in (4, 0, 4)], [banks[b] for b in (1, 2, 3)]
-        upper = [banks[b][:, 0:G] for b in (6, 5, 2)]
-        for c in range(GROUPS - E):
-            first, second, part, res = tiles("unit%d_" % c, 4, [P, G], F32)
-            tokens = slice(c * G, (c + 1) * G)
-            pick(first[:], 0, pos1_t, 0, tokens)
-            pick(second[:], 0, pos2_t, 1, tokens)
-            for block in blocks:
-                turn_and_add(there[c][:, block], (second[:, block], first[:, block]))
-            nc.scalar.copy(part[:], there[c][:, 0:G])
-            if c == GROUPS - E - 1:
-                second_shared(c, back[0])
-            for block in blocks:
-                turn_and_add(back[c][:, block], (part[:, block], shared[c][:, block]))
-            nc.scalar.copy(res[:], back[c][:, 0:G])
-            nc.sync.dma_start(out=out[0:P, tokens], in_=res[:])
+        units = {}
 
-        for c in range(GROUPS - E):
-            by_feature(upper[c], E + c, w2s[:, P:N].bitcast(FP8X4), s2s[:, 0, P:N])
-        first, second, part, res = tiles("late", 4, [P, T], F32)
-        for tokens in (slice(0, G), slice(G, T)):
-            pick(first[:, tokens], 1, pos1_t, 0, tokens)
-            pick(second[:, tokens], 1, pos2_t, 1, tokens)
-            thirds = range(tokens.start // G, tokens.stop // G)
-            for c in thirds:
-                third = slice(c * G, (c + 1) * G)
-                nc.vector.tensor_tensor(part[:, third], upper[c], first[:, third], ADD)
-            for c in thirds:
-                third = slice(c * G, (c + 1) * G)
-                nc.vector.tensor_tensor(res[:, third], part[:, third], second[:, third], ADD)
-                nc.sync.dma_start(out=out[P:N, third], in_=res[:, third])
+        def picks(v, c):
+            units[v, c] = tiles("unit%d%d_" % (v, c), 4, [P, G], F32)
+            tokens = slice(c * G, (c + 1) * G)
+            pick(units[v, c][0][:], v, pos1_t, 0, tokens)
+            pick(units[v, c][1][:], v, pos2_t, 1, tokens)
+
+        def there(v, c):
+            first, second, part, res = units[v, c]
+            bank = take(scalar_ring)
+            for block in blocks:
+                turn_and_add(bank[:, block], (second[:, block], first[:, block]))
+            nc.scalar.copy(part[:], bank[:, 0:G])
+
+        def back(v, c):
+            first, second, part, res = units[v, c]
+            bank = take(scalar_ring)
+            for j, block in enumerate(blocks):
+                turn_and_add(bank[:, block], (part[:, block], shared[c][:, j, v * P : (v + 1) * P]))
+            nc.scalar.copy(res[:], bank[:, 0:G])
+            nc.sync.dma_start(out=out[v * P : (v + 1) * P, c * G : (c + 1) * G], in_=res[:])
+
+        for e in range(0, E, 2):
+            gather(got_scales, xs[:, 0, :], "got_scales", e, 2)
+        for e in range(0, E, 2):
+            gather(got_words, xw[:].bitcast(U32), "got_words", e, 2)
+        for k in list(range(2 * E, 2 * GROUPS)) + list(range(4)):
+            gelu_side(k)
+        for k in range(len(vector_ring)):
+            gate_product(k)
+        for k in range(4, 2 * E):
+            gelu_side(k)
+        for k in range(7):
+            multiply(k)
+        turn([0, 1])
+        multiply(7)
+        turn([2, 3])
+        for k in range(8, 12):
+            multiply(k)
+        quantise(0)
+        quantise(1)
+        second_routed(0, [1, 0], scalar_ring)
+        turn([4, 5])
+        multiply(12)
+        quantise(2)
+        quantise(3)
+        second_routed(0, [3, 2], scalar_ring)
+        multiply(13)
+        multiply(14)
+        quantise(4)
+        quantise(5)
+        turn([6])
+        second_routed(0, [5, 4], scalar_ring)
+        multiply(15)
+        multiply(16)
+        multiply(17)
+        quantise(6)
+        turn([7, 8])
+        quantise(7)
+        quantise(8)
+        picks(0, 0)
+        second_shared(0, N)
+        second_routed(1, [0, 1], vector_ring)
+        there(0, 0)
+        picks(0, 1)
+        second_shared(1, P)
+        second_routed(1, [2, 3], vector_ring)
+        there(0, 1)
+        second_routed(1, [4, 5], vector_ring)
+        back(0, 0)
+        picks(0, 2)
+        second_shared(2, P)
+        there(0, 2)
+        back(0, 1)
+        picks(1, 0)
+        there(1, 0)
+        back(0, 2)
+        back(1, 0)
+        upper = take(vector_ring)
+        for c in (1, 2):
+            by_feature(upper[:, (c - 1) * G : c * G], E + c, w2s[:, P:N].bitcast(FP8X4), s2s[:, 0, P:N])
+        first, second, part, res = tiles("late", 4, [P, 2 * G], F32)
+        tokens = slice(G, T)
+        pick(first[:], 1, pos1_t, 0, tokens)
+        pick(second[:], 1, pos2_t, 1, tokens)
+        nc.vector.tensor_tensor(part[:], upper[:], first[:], ADD)
+        for c in (1, 2):
+            third = slice((c - 1) * G, c * G)
+            nc.vector.tensor_tensor(res[:, third], part[:, third], second[:, third], ADD)
+            nc.sync.dma_start(out=out[P:N, c * G : (c + 1) * G], in_=res[:, third])

@@ -79,7 +79,6 @@ def tile_moe_shf_glu_gelu_kernel(
 
         ports = (0, 2, 1, 3)
         nc.sync.dma_start(offs_t[:], offs)
-        nc.sync.dma_start(pos1_t[:], pos1)
         load_scales(nc.sync, (0, 2), xs[:], x_scales)
         load_scales(nc.scalar, (1, 3), xs[:], x_scales)
         load_fp8(nc.sync, xw, x_words)
@@ -89,8 +88,8 @@ def tile_moe_shf_glu_gelu_kernel(
         load_scales(nc.gpsimd, ports, s2[:], w2_scales[:, 0])
         make_identity(nc, ident[:])
         load_scales(nc.sync, ports, s1[:], w1_scales[:, 0])
-        load_fp4(nc.sync, w1_words, w1, "w1", 0, 2)
         load_scales(nc.sync, ports, s3[:], w3_scales[:, 0])
+        load_fp4(nc.sync, w1_words, w1, "w1", 0, 2)
         load_fp4(nc.sync, w3_words, w3, "w3", 0, 2)
         load_fp4(nc.sync, w1_words, w1, "w1", 2, 4)
         load_fp4(nc.sync, w1_words, w1, "w1", 4, 6)
@@ -101,6 +100,7 @@ def tile_moe_shf_glu_gelu_kernel(
         load_scales(nc.sync, ports, s3s[:], w3s_scales)
         load_fp8(nc.sync, w2s, w2s_words)
         load_scales(nc.sync, ports, s2s[:], w2s_scales)
+        nc.sync.dma_start(pos1_t[:], pos1)
         nc.sync.dma_start(pos2_t[:], pos2)
         nc.sync.dma_start(out=gate_t[:], in_=gate.rearrange("r p t -> p r t"))
 
@@ -150,7 +150,6 @@ def tile_moe_shf_glu_gelu_kernel(
 
         def multiply(k):
             nc.vector.tensor_tensor(hidden[k][:], gate_sums[k], acts[k][:], MULT)
-            gate_product(k + 4)
 
         def turn(groups):
             views = [take(scalar_ring)[:].rearrange("p (j u r) -> p j u r", j=2, u=2) for g in groups]
@@ -233,42 +232,83 @@ def tile_moe_shf_glu_gelu_kernel(
             gather(got_scales, xs[:, 0, :], "got_scales", e, 2)
         for e in range(0, E, 2):
             gather(got_words, xw[:].bitcast(U32), "got_words", e, 2)
-        for k in list(range(2 * E, 2 * GROUPS)) + list(range(4)):
-            gelu_side(k)
-        for k in range(len(vector_ring)):
-            gate_product(k)
-        for k in range(4, 2 * E):
-            gelu_side(k)
-        for k in range(7):
-            multiply(k)
-        turn([0, 1])
+        gelu_side(12)
+        gelu_side(13)
+        gelu_side(14)
+        gelu_side(15)
+        gelu_side(16)
+        gelu_side(17)
+        gelu_side(0)
+        gelu_side(1)
+        gate_product(0)
+        gelu_side(2)
+        gate_product(1)
+        gelu_side(3)
+        gate_product(2)
+        gelu_side(4)
+        gate_product(3)
+        multiply(0)
+        gelu_side(5)
+        gate_product(4)
+        multiply(1)
+        gelu_side(6)
+        gate_product(5)
+        multiply(2)
+        gelu_side(7)
+        gate_product(6)
+        multiply(3)
+        gelu_side(8)
+        gate_product(7)
+        multiply(4)
+        gelu_side(9)
+        gate_product(8)
+        multiply(5)
+        gelu_side(10)
+        gate_product(9)
+        multiply(6)
+        gelu_side(11)
+        gate_product(10)
+        turn([0])
         multiply(7)
-        turn([2, 3])
-        for k in range(8, 12):
-            multiply(k)
+        gate_product(11)
+        turn([1])
+        turn([2])
+        multiply(8)
+        multiply(9)
+        multiply(10)
+        multiply(11)
+        gate_product(12)
+        turn([3])
         quantise(0)
         quantise(1)
         second_routed(0, [1, 0], scalar_ring)
-        turn([4, 5])
+        gate_product(13)
+        turn([4])
         multiply(12)
         quantise(2)
+        gate_product(14)
+        turn([5])
         quantise(3)
         second_routed(0, [3, 2], scalar_ring)
         multiply(13)
-        multiply(14)
+        gate_product(15)
         quantise(4)
+        multiply(14)
+        gate_product(16)
         quantise(5)
         turn([6])
         second_routed(0, [5, 4], scalar_ring)
         multiply(15)
+        gate_product(17)
         multiply(16)
         multiply(17)
         quantise(6)
-        turn([7, 8])
+        turn([7])
+        turn([8])
         quantise(7)
         quantise(8)
         picks(0, 0)
-        second_shared(0, N)
+        second_shared(0, P)
         second_routed(1, [0, 1], vector_ring)
         there(0, 0)
         picks(0, 1)
@@ -281,19 +321,20 @@ def tile_moe_shf_glu_gelu_kernel(
         second_shared(2, P)
         there(0, 2)
         back(0, 1)
-        picks(1, 0)
-        there(1, 0)
         back(0, 2)
-        back(1, 0)
-        upper = take(vector_ring)
-        for c in (1, 2):
-            by_feature(upper[:, (c - 1) * G : c * G], E + c, w2s[:, P:N].bitcast(FP8X4), s2s[:, 0, P:N])
-        first, second, part, res = tiles("late", 4, [P, 2 * G], F32)
-        tokens = slice(G, T)
-        pick(first[:], 1, pos1_t, 0, tokens)
-        pick(second[:], 1, pos2_t, 1, tokens)
-        nc.vector.tensor_tensor(part[:], upper[:], first[:], ADD)
-        for c in (1, 2):
-            third = slice((c - 1) * G, c * G)
-            nc.vector.tensor_tensor(res[:, third], part[:, third], second[:, third], ADD)
-            nc.sync.dma_start(out=out[P:N, c * G : (c + 1) * G], in_=res[:, third])
+        pair, last = take(vector_ring), take(vector_ring)
+        upper = [pair[:, 0:G], pair[:, G:H], last[:, 0:G]]
+        for c in range(GROUPS - E):
+            by_feature(upper[c], E + c, w2s[:, P:N].bitcast(FP8X4), s2s[:, 0, P:N])
+        first, second, part, res = tiles("late", 4, [P, T], F32)
+        for tokens in (slice(0, G), slice(G, T)):
+            pick(first[:, tokens], 1, pos1_t, 0, tokens)
+            pick(second[:, tokens], 1, pos2_t, 1, tokens)
+            thirds = range(tokens.start // G, tokens.stop // G)
+            for c in thirds:
+                third = slice(c * G, (c + 1) * G)
+                nc.vector.tensor_tensor(part[:, third], upper[c], first[:, third], ADD)
+            for c in thirds:
+                third = slice(c * G, (c + 1) * G)
+                nc.vector.tensor_tensor(res[:, third], part[:, third], second[:, third], ADD)
+                nc.sync.dma_start(out=out[P:N, third], in_=res[:, third])

@@ -61,10 +61,10 @@ def tile_moe_shf_glu_gelu_kernel(
         gate_t = keep.tile([P, 2, T], F32, name="gate_t")
         ident = keep.tile([P, P], F32, name="ident")
 
-        for plane in (s2, s3, s3s, s2s):
-            nc.gpsimd.memset(plane[:].bitcast(I32), 0)
-        for plane in (xs, s1s, s1):
+        nc.gpsimd.memset(s2[:].bitcast(I32), 0)
+        for plane in (xs, s1s, s1, ident, s3, s3s, s2s):
             nc.vector.memset(plane[:].bitcast(I32), 0)
+        make_identity(nc, ident[:], nomemset=True)
 
         w1, w3, w2 = {}, {}, {}
 
@@ -85,8 +85,6 @@ def tile_moe_shf_glu_gelu_kernel(
         load_fp8(nc.sync, w1s, w1s_words)
         load_scales(nc.scalar, (0,), s1s[:], w1s_scales)
         load_scales(nc.sync, (2, 1, 3), s1s[:], w1s_scales)
-        load_scales(nc.gpsimd, ports, s2[:], w2_scales[:, 0])
-        make_identity(nc, ident[:])
         load_scales(nc.sync, ports, s1[:], w1_scales[:, 0])
         load_scales(nc.sync, ports, s3[:], w3_scales[:, 0])
         load_fp4(nc.sync, w1_words, w1, "w1", 0, 2)
@@ -95,29 +93,26 @@ def tile_moe_shf_glu_gelu_kernel(
         load_fp4(nc.sync, w1_words, w1, "w1", 4, 6)
         load_fp4(nc.sync, w3_words, w3, "w3", 2, 4)
         load_fp4(nc.sync, w3_words, w3, "w3", 4, 6)
-        load_fp4(nc.sync, w2_words, w2, "w2", 0, 6)
         load_fp8(nc.sync, w3s, w3s_words)
         load_scales(nc.sync, ports, s3s[:], w3s_scales)
+        load_fp4(nc.sync, w2_words, w2, "w2", 0, 6)
+        load_scales(nc.sync, ports, s2[:], w2_scales[:, 0])
         load_fp8(nc.sync, w2s, w2s_words)
-        load_scales(nc.sync, ports, s2s[:], w2s_scales)
         nc.sync.dma_start(pos1_t[:], pos1)
         nc.sync.dma_start(pos2_t[:], pos2)
-        nc.sync.dma_start(out=gate_t[:], in_=gate.rearrange("r p t -> p r t"))
+        gate_rows = gate.rearrange("r p t -> p r t")
+        nc.sync.dma_start(out=gate_t[:, :, 0 : 2 * G], in_=gate_rows[:, :, 0 : 2 * G])
+        load_scales(nc.sync, ports, s2s[:], w2s_scales)
+        nc.sync.dma_start(out=gate_t[:, :, 2 * G : T], in_=gate_rows[:, :, 2 * G : T])
 
         y = [keep.tile([P, S], F32, name="y%d" % v) for v in range(2)]
         banks = [psum.tile([P, H], F32, name="bank%d" % k) for k in range(8)]
-        scalar_ring = banks[0:4]
-        vector_ring = banks[4:8]
         got_words, got_scales, gate_sums = {}, {}, {}
         acts = tiles("act", 2 * GROUPS, [P, 2, P, 2], F32)
         hidden = tiles("h", 2 * GROUPS, [P, 2, P, 2], BF16)
         turned = tiles("ht", GROUPS, [P, 4 * G], BF16)
         codes = tiles("hq", GROUPS, [P, G], U32)
         code_scales = tiles("hs", GROUPS, [P, G], U8)
-
-        def take(ring):
-            ring[:] = ring[1:] + ring[:1]
-            return ring[-1]
 
         def gather(held, window, name, e, count):
             into = keep.tile([P, count * C], window.dtype, name="%s%d" % (name, e), align_bytes=64)
@@ -140,29 +135,25 @@ def tile_moe_shf_glu_gelu_kernel(
             )
             return acc[:].rearrange("p (m u e) -> p u m e", u=2, e=2)
 
-        def gelu_side(k):
-            sums = first_product(take(scalar_ring), k, w1, s1, w1s, s1s)
+        def gelu_side(k, bank):
+            sums = first_product(bank, k, w1, s1, w1s, s1s)
             nc.scalar.activation(acts[k][:], sums, GELU)
 
-        def gate_product(k):
-            if k < 2 * GROUPS:
-                gate_sums[k] = first_product(take(vector_ring), k, w3, s3, w3s, s3s)
+        def gate_product(k, bank):
+            gate_sums[k] = first_product(bank, k, w3, s3, w3s, s3s)
 
         def multiply(k):
             nc.vector.tensor_tensor(hidden[k][:], gate_sums[k], acts[k][:], MULT)
 
-        def turn(groups):
-            views = [take(scalar_ring)[:].rearrange("p (j u r) -> p j u r", j=2, u=2) for g in groups]
-            for g, tr in reversed(list(zip(groups, views))):
-                for j in (1, 0):
-                    pairs = hidden[2 * g + j][:].rearrange("p u m e -> p (u m e)").bitcast(F32)
-                    for u in range(2):
-                        nc.tensor.transpose(tr[:, j, u, :], pairs[:, u * P : (u + 1) * P], ident[:])
-            for g, tr in zip(groups, views):
-                nc.scalar.copy(
-                    turned[g][:].bitcast(F32).rearrange("p (j r u) -> p j r u", j=2, u=2),
-                    tr.rearrange("p j u r -> p j r u"),
-                )
+        def turn(g, bank):
+            tr = bank[:].rearrange("p (j u r) -> p j u r", j=2, u=2)
+            for j in (1, 0):
+                pairs = hidden[2 * g + j][:].rearrange("p u m e -> p (u m e)").bitcast(F32)
+                for u in range(2):
+                    nc.tensor.transpose(tr[:, j, u, :], pairs[:, u * P : (u + 1) * P], ident[:])
+            nc.scalar.copy(
+                turned[g][:].bitcast(F32).rearrange("p (j r u) -> p j r u", j=2, u=2), tr.rearrange("p j u r -> p j r u")
+            )
 
         def quantise(g):
             nc.vector.quantize_mx(out=codes[g][:].bitcast(FP8X4), scales=code_scales[g][:], in_=turned[g][:])
@@ -173,8 +164,7 @@ def tile_moe_shf_glu_gelu_kernel(
                 start=True, stop=True,
             )
 
-        def second_routed(v, experts, ring):
-            bank = take(ring)
+        def second_routed(v, experts, bank):
             cols = slice(v * P, (v + 1) * P)
             for g in experts:
                 w = w2[g][:, 2 * v * P : 2 * (v + 1) * P].bitcast(FP4X4)
@@ -184,8 +174,7 @@ def tile_moe_shf_glu_gelu_kernel(
 
         shared = {}
 
-        def second_shared(c, width):
-            bank = take(scalar_ring)
+        def second_shared(c, width, bank):
             for j in range(2):
                 nc.tensor.matmul_mx(
                     out=bank[:, j * width : (j + 1) * width],
@@ -213,16 +202,14 @@ def tile_moe_shf_glu_gelu_kernel(
             pick(units[v, c][0][:], v, pos1_t, 0, tokens)
             pick(units[v, c][1][:], v, pos2_t, 1, tokens)
 
-        def there(v, c):
+        def there(v, c, bank):
             first, second, part, res = units[v, c]
-            bank = take(scalar_ring)
             for block in blocks:
                 turn_and_add(bank[:, block], (second[:, block], first[:, block]))
             nc.scalar.copy(part[:], bank[:, 0:G])
 
-        def back(v, c):
+        def back(v, c, bank):
             first, second, part, res = units[v, c]
-            bank = take(scalar_ring)
             for j, block in enumerate(blocks):
                 turn_and_add(bank[:, block], (part[:, block], shared[c][:, j, v * P : (v + 1) * P]))
             nc.scalar.copy(res[:], bank[:, 0:G])
@@ -232,97 +219,97 @@ def tile_moe_shf_glu_gelu_kernel(
             gather(got_scales, xs[:, 0, :], "got_scales", e, 2)
         for e in range(0, E, 2):
             gather(got_words, xw[:].bitcast(U32), "got_words", e, 2)
-        gelu_side(12)
-        gelu_side(13)
-        gelu_side(14)
-        gelu_side(15)
-        gelu_side(16)
-        gelu_side(17)
-        gelu_side(0)
-        gelu_side(1)
-        gate_product(0)
-        gelu_side(2)
-        gate_product(1)
-        gelu_side(3)
-        gate_product(2)
-        gelu_side(4)
-        gate_product(3)
+        gelu_side(12, banks[0])
+        gelu_side(13, banks[1])
+        gelu_side(14, banks[2])
+        gelu_side(15, banks[3])
+        gelu_side(16, banks[0])
+        gelu_side(17, banks[1])
+        gelu_side(0, banks[2])
+        gelu_side(1, banks[3])
+        gate_product(0, banks[4])
+        gelu_side(2, banks[0])
+        gate_product(1, banks[5])
+        gelu_side(3, banks[1])
+        gate_product(2, banks[6])
+        gelu_side(4, banks[2])
+        gate_product(3, banks[7])
         multiply(0)
-        gelu_side(5)
-        gate_product(4)
+        gelu_side(5, banks[3])
+        gate_product(4, banks[4])
         multiply(1)
-        gelu_side(6)
-        gate_product(5)
+        gelu_side(6, banks[0])
+        gate_product(5, banks[5])
         multiply(2)
-        gelu_side(7)
-        gate_product(6)
+        gelu_side(7, banks[1])
+        gate_product(6, banks[6])
         multiply(3)
-        gelu_side(8)
-        gate_product(7)
+        gelu_side(8, banks[2])
+        gate_product(7, banks[7])
         multiply(4)
-        gelu_side(9)
-        gate_product(8)
+        gelu_side(9, banks[3])
+        gate_product(8, banks[4])
         multiply(5)
-        gelu_side(10)
-        gate_product(9)
+        gelu_side(10, banks[0])
+        gate_product(9, banks[5])
         multiply(6)
-        gelu_side(11)
-        gate_product(10)
-        turn([0])
+        gelu_side(11, banks[1])
+        gate_product(10, banks[6])
         multiply(7)
-        gate_product(11)
-        turn([1])
-        turn([2])
+        gate_product(11, banks[7])
+        turn(0, banks[2])
+        turn(1, banks[3])
         multiply(8)
+        gate_product(12, banks[4])
         multiply(9)
+        gate_product(13, banks[5])
         multiply(10)
+        gate_product(14, banks[6])
+        turn(2, banks[0])
+        turn(3, banks[1])
         multiply(11)
-        gate_product(12)
-        turn([3])
+        gate_product(15, banks[7])
         quantise(0)
         quantise(1)
-        second_routed(0, [1, 0], scalar_ring)
-        gate_product(13)
-        turn([4])
+        second_routed(0, [1, 0], banks[2])
         multiply(12)
+        gate_product(16, banks[4])
+        turn(4, banks[3])
+        turn(5, banks[0])
         quantise(2)
-        gate_product(14)
-        turn([5])
         quantise(3)
-        second_routed(0, [3, 2], scalar_ring)
+        second_routed(0, [3, 2], banks[1])
         multiply(13)
-        gate_product(15)
+        gate_product(17, banks[5])
         quantise(4)
         multiply(14)
-        gate_product(16)
         quantise(5)
-        turn([6])
-        second_routed(0, [5, 4], scalar_ring)
+        second_routed(0, [5, 4], banks[3])
+        turn(6, banks[2])
         multiply(15)
-        gate_product(17)
         multiply(16)
         multiply(17)
         quantise(6)
-        turn([7])
-        turn([8])
-        quantise(7)
-        quantise(8)
+        turn(7, banks[0])
         picks(0, 0)
-        second_shared(0, P)
-        second_routed(1, [0, 1], vector_ring)
-        there(0, 0)
+        quantise(7)
+        turn(8, banks[1])
+        second_shared(0, P, banks[2])
+        second_routed(1, [0, 1], banks[6])
+        second_routed(1, [2, 3], banks[7])
+        second_routed(1, [4, 5], banks[4])
+        there(0, 0, banks[3])
         picks(0, 1)
-        second_shared(1, P)
-        second_routed(1, [2, 3], vector_ring)
-        there(0, 1)
-        second_routed(1, [4, 5], vector_ring)
-        back(0, 0)
+        quantise(8)
+        second_shared(1, P, banks[0])
+        there(0, 1, banks[1])
+        back(0, 0, banks[2])
         picks(0, 2)
-        second_shared(2, P)
-        there(0, 2)
-        back(0, 1)
-        back(0, 2)
-        pair, last = take(vector_ring), take(vector_ring)
+        second_shared(2, P, banks[3])
+        there(0, 2, banks[0])
+        back(0, 1, banks[1])
+        back(0, 2, banks[2])
+        pair, last = banks[5], banks[6]
         upper = [pair[:, 0:G], pair[:, G:H], last[:, 0:G]]
         for c in range(GROUPS - E):
             by_feature(upper[c], E + c, w2s[:, P:N].bitcast(FP8X4), s2s[:, 0, P:N])

@@ -77,6 +77,10 @@ def tile_moe_shf_glu_gelu_kernel(
         def load_fp8(queue, t, words):
             queue.dma_start(out=t[:], in_=words[0].rearrange("p n d -> p (n d)").bitcast(I32))
 
+        def load_gate(c):
+            third = slice(c * G, (c + 1) * G)
+            nc.sync.dma_start(out=gate_t[:, :, third], in_=gate.rearrange("r p t -> p r t")[:, :, third])
+
         ports = (0, 2, 1, 3)
         nc.sync.dma_start(offs_t[:], offs)
         load_scales(nc.sync, (0, 2), xs[:], x_scales)
@@ -87,6 +91,8 @@ def tile_moe_shf_glu_gelu_kernel(
         load_scales(nc.sync, (2, 1, 3), s1s[:], w1s_scales)
         load_scales(nc.sync, ports, s1[:], w1_scales[:, 0])
         load_scales(nc.sync, ports, s3[:], w3_scales[:, 0])
+        nc.sync.dma_start(pos1_t[:], pos1)
+        nc.sync.dma_start(pos2_t[:], pos2)
         load_fp4(nc.sync, w1_words, w1, "w1", 0, 2)
         load_fp4(nc.sync, w3_words, w3, "w3", 0, 2)
         load_fp4(nc.sync, w1_words, w1, "w1", 2, 4)
@@ -98,12 +104,10 @@ def tile_moe_shf_glu_gelu_kernel(
         load_fp4(nc.sync, w2_words, w2, "w2", 0, 6)
         load_scales(nc.sync, ports, s2[:], w2_scales[:, 0])
         load_fp8(nc.sync, w2s, w2s_words)
-        nc.sync.dma_start(pos1_t[:], pos1)
-        nc.sync.dma_start(pos2_t[:], pos2)
-        gate_rows = gate.rearrange("r p t -> p r t")
-        nc.sync.dma_start(out=gate_t[:, :, 0 : 2 * G], in_=gate_rows[:, :, 0 : 2 * G])
+        load_gate(0)
         load_scales(nc.sync, ports, s2s[:], w2s_scales)
-        nc.sync.dma_start(out=gate_t[:, :, 2 * G : T], in_=gate_rows[:, :, 2 * G : T])
+        load_gate(1)
+        load_gate(2)
 
         y = [keep.tile([P, S], F32, name="y%d" % v) for v in range(2)]
         banks = [psum.tile([P, H], F32, name="bank%d" % k) for k in range(8)]
@@ -193,6 +197,10 @@ def tile_moe_shf_glu_gelu_kernel(
             for k, term in enumerate(terms):
                 nc.tensor.matmul(into, term, ident[:], start=(k == 0), stop=(k == len(terms) - 1), is_transpose=True)
 
+        def keep_clock_up(bank):
+            for k in range(2):
+                first_product(bank, 2 * E + k, w1, s1, w1s, s1s)
+
         blocks = [slice(j * P, (j + 1) * P) for j in range(2)]
         units = {}
 
@@ -213,7 +221,7 @@ def tile_moe_shf_glu_gelu_kernel(
             for j, block in enumerate(blocks):
                 turn_and_add(bank[:, block], (part[:, block], shared[c][:, j, v * P : (v + 1) * P]))
             nc.scalar.copy(res[:], bank[:, 0:G])
-            nc.sync.dma_start(out=out[v * P : (v + 1) * P, c * G : (c + 1) * G], in_=res[:])
+            nc.scalar.dma_start(out=out[v * P : (v + 1) * P, c * G : (c + 1) * G], in_=res[:])
 
         for e in range(0, E, 2):
             gather(got_scales, xs[:, 0, :], "got_scales", e, 2)
@@ -291,37 +299,41 @@ def tile_moe_shf_glu_gelu_kernel(
         multiply(17)
         quantise(6)
         turn(7, banks[0])
-        picks(0, 0)
         quantise(7)
         turn(8, banks[1])
-        second_shared(0, P, banks[2])
+        picks(0, 0)
+        quantise(8)
+        second_shared(0, N, banks[2])
+        second_shared(1, P, banks[0])
+        keep_clock_up(banks[3])
+        there(0, 0, banks[3])
         second_routed(1, [0, 1], banks[6])
         second_routed(1, [2, 3], banks[7])
+        back(0, 0, banks[0])
         second_routed(1, [4, 5], banks[4])
-        there(0, 0, banks[3])
         picks(0, 1)
-        quantise(8)
-        second_shared(1, P, banks[0])
-        there(0, 1, banks[1])
-        back(0, 0, banks[2])
+        keep_clock_up(banks[6])
+        there(0, 1, banks[6])
+        second_shared(2, P, banks[1])
+        upper = banks[5]
+        for c in (1, 2):
+            by_feature(upper[:, (c - 1) * G : c * G], E + c, w2s[:, P:N].bitcast(FP8X4), s2s[:, 0, P:N])
         picks(0, 2)
-        second_shared(2, P, banks[3])
-        there(0, 2, banks[0])
-        back(0, 1, banks[1])
-        back(0, 2, banks[2])
-        pair, last = banks[5], banks[6]
-        upper = [pair[:, 0:G], pair[:, G:H], last[:, 0:G]]
-        for c in range(GROUPS - E):
-            by_feature(upper[c], E + c, w2s[:, P:N].bitcast(FP8X4), s2s[:, 0, P:N])
-        first, second, part, res = tiles("late", 4, [P, T], F32)
-        for tokens in (slice(0, G), slice(G, T)):
-            pick(first[:, tokens], 1, pos1_t, 0, tokens)
-            pick(second[:, tokens], 1, pos2_t, 1, tokens)
-            thirds = range(tokens.start // G, tokens.stop // G)
-            for c in thirds:
-                third = slice(c * G, (c + 1) * G)
-                nc.vector.tensor_tensor(part[:, third], upper[c], first[:, third], ADD)
-            for c in thirds:
-                third = slice(c * G, (c + 1) * G)
-                nc.vector.tensor_tensor(res[:, third], part[:, third], second[:, third], ADD)
-                nc.sync.dma_start(out=out[P:N, third], in_=res[:, third])
+        back(0, 1, banks[3])
+        keep_clock_up(banks[2])
+        there(0, 2, banks[2])
+        picks(1, 0)
+        keep_clock_up(banks[4])
+        there(1, 0, banks[4])
+        back(0, 2, banks[6])
+        back(1, 0, banks[0])
+        first, second, part, res = tiles("late", 4, [P, 2 * G], F32)
+        tokens = slice(G, T)
+        pick(first[:], 1, pos1_t, 0, tokens)
+        pick(second[:], 1, pos2_t, 1, tokens)
+        halves = [slice(0, G), slice(G, 2 * G)]
+        for half in halves:
+            nc.vector.tensor_tensor(part[:, half], upper[:, half], first[:, half], ADD)
+        for c, half in zip((1, 2), halves):
+            nc.vector.tensor_tensor(res[:, half], part[:, half], second[:, half], ADD)
+            nc.sync.dma_start(out=out[P:N, c * G : (c + 1) * G], in_=res[:, half])

@@ -21,6 +21,7 @@ ADD = mybir.AluOpType.add
 
 P = 128
 G = 256
+UPPER_BLOCKS = 3
 GROUPS = E + T // G
 
 
@@ -111,12 +112,17 @@ def tile_moe_shf_glu_gelu_kernel(
 
         y = [keep.tile([P, S], F32, name="y%d" % v) for v in range(2)]
         banks = [psum.tile([P, H], F32, name="bank%d" % k) for k in range(8)]
-        got_words, got_scales, gate_sums = {}, {}, {}
+        scalar_ring, vector_ring = banks[0:4], banks[4:8]
+        got_words, got_scales, gate_sums, shared, units = {}, {}, {}, {}, {}
         acts = tiles("act", 2 * GROUPS, [P, 2, P, 2], F32)
         hidden = tiles("h", 2 * GROUPS, [P, 2, P, 2], BF16)
         turned = tiles("ht", GROUPS, [P, 4 * G], BF16)
         codes = tiles("hq", GROUPS, [P, G], U32)
         code_scales = tiles("hs", GROUPS, [P, G], U8)
+
+        def take(ring):
+            ring[:] = ring[1:] + ring[:1]
+            return ring[-1]
 
         def gather(held, window, name, e, count):
             into = keep.tile([P, count * C], window.dtype, name="%s%d" % (name, e), align_bytes=64)
@@ -124,10 +130,10 @@ def tile_moe_shf_glu_gelu_kernel(
             for i in range(count):
                 held[e + i] = into[:, i * C : (i + 1) * C]
 
-        def first_product(acc, k, routed, routed_scales, common, common_scales):
+        def first_product(bank, k, routed, routed_scales, common, common_scales):
             g, j = divmod(k, 2)
-            cols = slice(j * P, (j + 1) * P)
             if g < E:
+                cols = slice(j * P, (j + 1) * P)
                 words, scales = got_words[g][:, cols], got_scales[g][:, cols]
                 w, ws = routed[g].bitcast(FP4X4), routed_scales[:, g, :]
             else:
@@ -135,19 +141,23 @@ def tile_moe_shf_glu_gelu_kernel(
                 words, scales = xw[:, cols], xs[:, 0, cols]
                 w, ws = common[:].bitcast(FP8X4), common_scales[:, 0, :]
             nc.tensor.matmul_mx(
-                out=acc[:], lhsT=words.bitcast(FP8X4), lhsT_scale=scales, rhs=w, rhs_scale=ws, start=True, stop=True
+                out=bank[:], lhsT=words.bitcast(FP8X4), lhsT_scale=scales, rhs=w, rhs_scale=ws, start=True, stop=True
             )
-            return acc[:].rearrange("p (m u e) -> p u m e", u=2, e=2)
+            return bank[:].rearrange("p (m u e) -> p u m e", u=2, e=2)
 
-        def gelu_side(k, bank):
-            sums = first_product(bank, k, w1, s1, w1s, s1s)
+        def gelu_side(k):
+            sums = first_product(take(scalar_ring), k, w1, s1, w1s, s1s)
             nc.scalar.activation(acts[k][:], sums, GELU)
 
-        def gate_product(k, bank):
-            gate_sums[k] = first_product(bank, k, w3, s3, w3s, s3s)
+        def gate_side(k):
+            gate_sums[k] = first_product(take(vector_ring), k, w3, s3, w3s, s3s)
 
         def multiply(k):
             nc.vector.tensor_tensor(hidden[k][:], gate_sums[k], acts[k][:], MULT)
+
+        def multiply_and_refill(k):
+            multiply(k)
+            gate_side(k + len(vector_ring))
 
         def turn(g, bank):
             tr = bank[:].rearrange("p (j u r) -> p j u r", j=2, u=2)
@@ -162,36 +172,38 @@ def tile_moe_shf_glu_gelu_kernel(
         def quantise(g):
             nc.vector.quantize_mx(out=codes[g][:].bitcast(FP8X4), scales=code_scales[g][:], in_=turned[g][:])
 
-        def by_feature(acc, g, w, ws):
+        def by_feature(acc, g, cols, w, ws):
             nc.tensor.matmul_mx(
-                out=acc, lhsT=w, lhsT_scale=ws, rhs=codes[g][:].bitcast(FP8X4), rhs_scale=code_scales[g][:],
+                out=acc, lhsT=w, lhsT_scale=ws, rhs=codes[g][:, cols].bitcast(FP8X4), rhs_scale=code_scales[g][:, cols],
                 start=True, stop=True,
             )
 
         def second_routed(v, experts, bank):
-            cols = slice(v * P, (v + 1) * P)
+            low = min(experts)
             for g in experts:
                 w = w2[g][:, 2 * v * P : 2 * (v + 1) * P].bitcast(FP4X4)
-                i = g - min(experts)
-                by_feature(bank[:, i * G : (i + 1) * G], g, w, s2[:, g, cols])
-            nc.scalar.copy(y[v][:, min(experts) * C : (max(experts) + 1) * C], bank[:, 0 : len(experts) * G])
+                by_feature(bank[:, (g - low) * G : (g - low + 1) * G], g, slice(0, G), w, s2[:, g, v * P : (v + 1) * P])
+            nc.scalar.copy(y[v][:, low * C : (low + 2) * C], bank[:])
 
-        shared = {}
-
-        def second_shared(c, width, bank):
-            for j in range(2):
+        def second_shared(c, bank):
+            widths = [N if b < UPPER_BLOCKS else P for b in (2 * c, 2 * c + 1)]
+            held = keep.tile([P, sum(widths)], F32, name="shared%d" % c)
+            for j, width in enumerate(widths):
+                cols = slice(j * widths[0], j * widths[0] + width)
                 nc.tensor.matmul_mx(
-                    out=bank[:, j * width : (j + 1) * width],
-                    lhsT=codes[E + c][:, j * P : (j + 1) * P].bitcast(FP8X4),
+                    out=bank[:, cols], lhsT=codes[E + c][:, j * P : (j + 1) * P].bitcast(FP8X4),
                     lhsT_scale=code_scales[E + c][:, j * P : (j + 1) * P],
                     rhs=w2s[:, 0:width].bitcast(FP8X4), rhs_scale=s2s[:, 0, 0:width], start=True, stop=True,
                 )
-            shared[c] = keep.tile([P, 2, width], F32, name="shared%d" % c)
-            nc.scalar.copy(shared[c][:].rearrange("p j w -> p (j w)"), bank[:, 0 : 2 * width])
+                shared[2 * c + j] = held[:, cols]
+            nc.scalar.copy(held[:], bank[:, 0 : sum(widths)])
 
-        def pick(into, v, places, r, tokens):
-            window = y[v][:].indirect(places[:, tokens.start // 16 : tokens.stop // 16])
-            nc.vector.tensor_tensor(into, window, gate_t[:, r, tokens], MULT)
+        def picks(name, v, tokens):
+            first, second, part, res = tiles(name, 4, [P, tokens.stop - tokens.start], F32)
+            for r, (into, places) in enumerate(((first, pos1_t), (second, pos2_t))):
+                window = y[v][:].indirect(places[:, tokens.start // 16 : tokens.stop // 16])
+                nc.vector.tensor_tensor(into[:], window, gate_t[:, r, tokens], MULT)
+            return first, second, part, res
 
         def turn_and_add(into, terms):
             for k, term in enumerate(terms):
@@ -201,139 +213,96 @@ def tile_moe_shf_glu_gelu_kernel(
             for k in range(2):
                 first_product(bank, 2 * E + k, w1, s1, w1s, s1s)
 
-        blocks = [slice(j * P, (j + 1) * P) for j in range(2)]
-        units = {}
+        def there(v, tokens, bank):
+            first, second, part, res = units[v, tokens.start]
+            width = tokens.stop - tokens.start
+            for col in range(0, width, P):
+                turn_and_add(bank[:, col : col + P], (second[:, col : col + P], first[:, col : col + P]))
+            nc.scalar.copy(part[:], bank[:, 0:width])
 
-        def picks(v, c):
-            units[v, c] = tiles("unit%d%d_" % (v, c), 4, [P, G], F32)
-            tokens = slice(c * G, (c + 1) * G)
-            pick(units[v, c][0][:], v, pos1_t, 0, tokens)
-            pick(units[v, c][1][:], v, pos2_t, 1, tokens)
-
-        def there(v, c, bank):
-            first, second, part, res = units[v, c]
-            for block in blocks:
-                turn_and_add(bank[:, block], (second[:, block], first[:, block]))
-            nc.scalar.copy(part[:], bank[:, 0:G])
-
-        def back(v, c, bank):
-            first, second, part, res = units[v, c]
-            for j, block in enumerate(blocks):
-                turn_and_add(bank[:, block], (part[:, block], shared[c][:, j, v * P : (v + 1) * P]))
-            nc.scalar.copy(res[:], bank[:, 0:G])
-            nc.scalar.dma_start(out=out[v * P : (v + 1) * P, c * G : (c + 1) * G], in_=res[:])
+        def back(v, tokens, bank):
+            first, second, part, res = units[v, tokens.start]
+            width = tokens.stop - tokens.start
+            for col in range(0, width, P):
+                ys = shared[(tokens.start + col) // P][:, v * P : (v + 1) * P]
+                turn_and_add(bank[:, col : col + P], (part[:, col : col + P], ys))
+            nc.scalar.copy(res[:], bank[:, 0:width])
+            nc.scalar.dma_start(out=out[v * P : (v + 1) * P, tokens], in_=res[:])
 
         for e in range(0, E, 2):
             gather(got_scales, xs[:, 0, :], "got_scales", e, 2)
         for e in range(0, E, 2):
             gather(got_words, xw[:].bitcast(U32), "got_words", e, 2)
-        gelu_side(12, banks[0])
-        gelu_side(13, banks[1])
-        gelu_side(14, banks[2])
-        gelu_side(15, banks[3])
-        gelu_side(16, banks[0])
-        gelu_side(17, banks[1])
-        gelu_side(0, banks[2])
-        gelu_side(1, banks[3])
-        gate_product(0, banks[4])
-        gelu_side(2, banks[0])
-        gate_product(1, banks[5])
-        gelu_side(3, banks[1])
-        gate_product(2, banks[6])
-        gelu_side(4, banks[2])
-        gate_product(3, banks[7])
-        multiply(0)
-        gelu_side(5, banks[3])
-        gate_product(4, banks[4])
-        multiply(1)
-        gelu_side(6, banks[0])
-        gate_product(5, banks[5])
-        multiply(2)
-        gelu_side(7, banks[1])
-        gate_product(6, banks[6])
-        multiply(3)
-        gelu_side(8, banks[2])
-        gate_product(7, banks[7])
-        multiply(4)
-        gelu_side(9, banks[3])
-        gate_product(8, banks[4])
-        multiply(5)
-        gelu_side(10, banks[0])
-        gate_product(9, banks[5])
-        multiply(6)
-        gelu_side(11, banks[1])
-        gate_product(10, banks[6])
-        multiply(7)
-        gate_product(11, banks[7])
-        turn(0, banks[2])
-        turn(1, banks[3])
-        multiply(8)
-        gate_product(12, banks[4])
-        multiply(9)
-        gate_product(13, banks[5])
-        multiply(10)
-        gate_product(14, banks[6])
-        turn(2, banks[0])
-        turn(3, banks[1])
-        multiply(11)
-        gate_product(15, banks[7])
+
+        for k in list(range(2 * E, 2 * GROUPS)) + [0, 1]:
+            gelu_side(k)
+        for k in range(2 * E - 1):
+            if k >= len(vector_ring):
+                multiply(k - len(vector_ring))
+            if k > 0:
+                gelu_side(k + 1)
+            gate_side(k)
+        multiply_and_refill(7)
+        turn(0, take(scalar_ring))
+        turn(1, take(scalar_ring))
+        for k in (8, 9, 10):
+            multiply_and_refill(k)
+        turn(2, take(scalar_ring))
+        turn(3, take(scalar_ring))
+        multiply_and_refill(11)
         quantise(0)
         quantise(1)
-        second_routed(0, [1, 0], banks[2])
-        multiply(12)
-        gate_product(16, banks[4])
-        turn(4, banks[3])
-        turn(5, banks[0])
+        second_routed(0, (1, 0), take(scalar_ring))
+        multiply_and_refill(12)
+        turn(4, take(scalar_ring))
+        turn(5, take(scalar_ring))
         quantise(2)
         quantise(3)
-        second_routed(0, [3, 2], banks[1])
-        multiply(13)
-        gate_product(17, banks[5])
+        second_routed(0, (3, 2), take(scalar_ring))
+        multiply_and_refill(13)
         quantise(4)
         multiply(14)
         quantise(5)
-        second_routed(0, [5, 4], banks[3])
-        turn(6, banks[2])
-        multiply(15)
-        multiply(16)
-        multiply(17)
-        quantise(6)
-        turn(7, banks[0])
-        quantise(7)
-        turn(8, banks[1])
-        picks(0, 0)
-        quantise(8)
-        second_shared(0, N, banks[2])
-        second_shared(1, P, banks[0])
-        keep_clock_up(banks[3])
-        there(0, 0, banks[3])
-        second_routed(1, [0, 1], banks[6])
-        second_routed(1, [2, 3], banks[7])
-        back(0, 0, banks[0])
-        second_routed(1, [4, 5], banks[4])
-        picks(0, 1)
-        keep_clock_up(banks[6])
-        there(0, 1, banks[6])
-        second_shared(2, P, banks[1])
-        upper = banks[5]
-        for c in (1, 2):
-            by_feature(upper[:, (c - 1) * G : c * G], E + c, w2s[:, P:N].bitcast(FP8X4), s2s[:, 0, P:N])
-        picks(0, 2)
-        back(0, 1, banks[3])
-        keep_clock_up(banks[2])
-        there(0, 2, banks[2])
-        picks(1, 0)
-        keep_clock_up(banks[4])
-        there(1, 0, banks[4])
-        back(0, 2, banks[6])
-        back(1, 0, banks[0])
-        first, second, part, res = tiles("late", 4, [P, 2 * G], F32)
-        tokens = slice(G, T)
-        pick(first[:], 1, pos1_t, 0, tokens)
-        pick(second[:], 1, pos2_t, 1, tokens)
-        halves = [slice(0, G), slice(G, 2 * G)]
-        for half in halves:
-            nc.vector.tensor_tensor(part[:, half], upper[:, half], first[:, half], ADD)
-        for c, half in zip((1, 2), halves):
-            nc.vector.tensor_tensor(res[:, half], part[:, half], second[:, half], ADD)
-            nc.sync.dma_start(out=out[P:N, c * G : (c + 1) * G], in_=res[:, half])
+        first_third, last_pair = take(scalar_ring), take(scalar_ring)
+        second_routed(0, (5, 4), last_pair)
+        turn(E, first_third)
+        for k in (15, 16, 17):
+            multiply(k)
+        quantise(E)
+        for g in (E + 1, E + 2):
+            turn(g, take(scalar_ring))
+            quantise(g)
+
+        by_vector = slice(UPPER_BLOCKS * P, T)
+        stretches = [(0, slice(c * G, (c + 1) * G)) for c in range(T // G)]
+        stretches = stretches + [(1, slice(0, G))] + [(1, slice(t, t + P)) for t in range(G, by_vector.start, P)]
+        for i, (v, tokens) in enumerate(stretches):
+            units[v, tokens.start] = picks("unit%d_" % i, v, tokens)
+            if v == 0:
+                second_shared(i, take(scalar_ring))
+            if i == T // G - 1:
+                upper = take(vector_ring)
+                pieces = []
+                for t in range(by_vector.start, T, P):
+                    if t % G == 0 or t == by_vector.start:
+                        stop = (t // G + 1) * G
+                        cols = slice(t - by_vector.start, stop - by_vector.start)
+                        by_feature(upper[:, cols], E + t // G, slice(t % G, G), w2s[:, P:N].bitcast(FP8X4), s2s[:, 0, P:N])
+                        pieces.append((cols, slice(t, stop)))
+            bank = take(scalar_ring)
+            if i < 4:
+                keep_clock_up(bank)
+            there(v, tokens, bank)
+            if i == 0:
+                for e in range(0, E, 2):
+                    second_routed(1, (e, e + 1), take(vector_ring))
+            else:
+                back(*stretches[i - 1], take(scalar_ring))
+        back(*stretches[-1], take(scalar_ring))
+
+        first, second, part, res = picks("late", 1, by_vector)
+        for cols, tokens in reversed(pieces):
+            nc.vector.tensor_tensor(part[:, cols], upper[:, cols], first[:, cols], ADD)
+        for cols, tokens in reversed(pieces):
+            nc.vector.tensor_tensor(res[:, cols], part[:, cols], second[:, cols], ADD)
+            nc.sync.dma_start(out=out[P:N, tokens], in_=res[:, cols])

@@ -92,8 +92,6 @@ def tile_moe_shf_glu_gelu_kernel(
         load_scales(nc.sync, (2, 1, 3), s1s[:], w1s_scales)
         load_scales(nc.sync, ports, s1[:], w1_scales[:, 0])
         load_scales(nc.sync, ports, s3[:], w3_scales[:, 0])
-        nc.sync.dma_start(pos1_t[:], pos1)
-        nc.sync.dma_start(pos2_t[:], pos2)
         load_fp4(nc.sync, w1_words, w1, "w1", 0, 2)
         load_fp4(nc.sync, w3_words, w3, "w3", 0, 2)
         load_fp4(nc.sync, w1_words, w1, "w1", 2, 4)
@@ -105,6 +103,8 @@ def tile_moe_shf_glu_gelu_kernel(
         load_fp4(nc.sync, w2_words, w2, "w2", 0, 6)
         load_scales(nc.sync, ports, s2[:], w2_scales[:, 0])
         load_fp8(nc.sync, w2s, w2s_words)
+        nc.sync.dma_start(pos1_t[:], pos1)
+        nc.sync.dma_start(pos2_t[:], pos2)
         load_gate(0)
         load_scales(nc.sync, ports, s2s[:], w2s_scales)
         load_gate(1)
@@ -145,8 +145,8 @@ def tile_moe_shf_glu_gelu_kernel(
             )
             return bank[:].rearrange("p (m u e) -> p u m e", u=2, e=2)
 
-        def gelu_side(k):
-            sums = first_product(take(scalar_ring), k, w1, s1, w1s, s1s)
+        def gelu_side(k, ring=scalar_ring):
+            sums = first_product(take(ring), k, w1, s1, w1s, s1s)
             nc.scalar.activation(acts[k][:], sums, GELU)
 
         def gate_side(k):
@@ -234,8 +234,8 @@ def tile_moe_shf_glu_gelu_kernel(
         for e in range(0, E, 2):
             gather(got_words, xw[:].bitcast(U32), "got_words", e, 2)
 
-        for k in list(range(2 * E, 2 * GROUPS)) + [0, 1]:
-            gelu_side(k)
+        for i, k in enumerate(list(range(2 * E, 2 * GROUPS)) + [0, 1]):
+            gelu_side(k, scalar_ring if i < len(scalar_ring) else vector_ring)
         for k in range(2 * E - 1):
             if k >= len(vector_ring):
                 multiply(k - len(vector_ring))

@@ -115,8 +115,10 @@ def tile_moe_shf_glu_gelu_kernel(
         scalar_ring, vector_ring = banks[0:4], banks[4:8]
         got_words, got_scales, gate_sums, shared, units = {}, {}, {}, {}, {}
         acts = tiles("act", 2 * GROUPS, [P, 2, P, 2], F32)
-        hidden = tiles("h", 2 * GROUPS, [P, 2, P, 2], BF16)
         turned = tiles("ht", GROUPS, [P, 4 * G], BF16)
+        hidden = [t[:] for t in tiles("h", 2 * GROUPS - 3, [P, H], BF16)]
+        spent = acts[len(hidden)][:].rearrange("p u m e -> p (u m e)").bitcast(BF16)
+        hidden = hidden + [turned[E - 1][:, 0:H], turned[E - 1][:, H : 2 * H], spent[:, 0:H]]
         codes = tiles("hq", GROUPS, [P, G], U32)
         code_scales = tiles("hs", GROUPS, [P, G], U8)
 
@@ -153,7 +155,8 @@ def tile_moe_shf_glu_gelu_kernel(
             gate_sums[k] = first_product(take(vector_ring), k, w3, s3, w3s, s3s)
 
         def multiply(k):
-            nc.vector.tensor_tensor(hidden[k][:], gate_sums[k], acts[k][:], MULT)
+            into = hidden[k].rearrange("p (u m e) -> p u m e", u=2, e=2)
+            nc.vector.tensor_tensor(into, gate_sums[k], acts[k][:], MULT)
 
         def multiply_and_refill(k):
             multiply(k)
@@ -162,7 +165,7 @@ def tile_moe_shf_glu_gelu_kernel(
         def turn(g, bank):
             tr = bank[:].rearrange("p (j u r) -> p j u r", j=2, u=2)
             for j in (1, 0):
-                pairs = hidden[2 * g + j][:].rearrange("p u m e -> p (u m e)").bitcast(F32)
+                pairs = hidden[2 * g + j].bitcast(F32)
                 for u in range(2):
                     nc.tensor.transpose(tr[:, j, u, :], pairs[:, u * P : (u + 1) * P], ident[:])
             nc.scalar.copy(
@@ -252,26 +255,20 @@ def tile_moe_shf_glu_gelu_kernel(
         multiply_and_refill(11)
         quantise(0)
         quantise(1)
-        second_routed(0, (1, 0), take(scalar_ring))
         multiply_and_refill(12)
         turn(4, take(scalar_ring))
         turn(5, take(scalar_ring))
         quantise(2)
         quantise(3)
-        second_routed(0, (3, 2), take(scalar_ring))
         multiply_and_refill(13)
         quantise(4)
-        multiply(14)
         quantise(5)
-        first_third, last_pair = take(scalar_ring), take(scalar_ring)
-        second_routed(0, (5, 4), last_pair)
-        turn(E, first_third)
-        for k in (15, 16, 17):
+        for g in range(0, E, 2):
+            second_routed(0, (g + 1, g), take(scalar_ring))
+        for k in (14, 15, 16, 17):
             multiply(k)
-        quantise(E)
-        for g in (E + 1, E + 2):
+        for g in range(E, GROUPS):
             turn(g, take(scalar_ring))
-            quantise(g)
 
         by_vector = slice(UPPER_BLOCKS * P, T)
         stretches = [(0, slice(c * G, (c + 1) * G)) for c in range(T // G)]
@@ -279,6 +276,7 @@ def tile_moe_shf_glu_gelu_kernel(
         for i, (v, tokens) in enumerate(stretches):
             units[v, tokens.start] = picks("unit%d_" % i, v, tokens)
             if v == 0:
+                quantise(E + i)
                 second_shared(i, take(scalar_ring))
             if i == T // G - 1:
                 upper = take(vector_ring)

from contextlib import ExitStack

import concourse.mybir as mybir
from concourse.masks import make_identity

K, T, E, C, H, N = 512, 768, 6, 256, 512, 256
S = E * C
FLOPS = 2 * (S + T) * (2 * K * H + H * N)

F32 = mybir.dt.float32
BF16 = mybir.dt.bfloat16
I32 = mybir.dt.int32
U32 = mybir.dt.uint32
U16 = mybir.dt.uint16
U8 = mybir.dt.uint8
FP8X4 = mybir.dt.float8_e4m3fn_x4
FP4X4 = mybir.dt.float4_e2m1fn_x4
GELU = mybir.ActivationFunctionType.Gelu_apprx_tanh
MULT = mybir.AluOpType.mult
ADD = mybir.AluOpType.add

P = 128
G = 256
UPPER_BLOCKS = 3
GROUPS = E + T // G


def load_scales(queue, quadrants, plane, scales):
    for q in quadrants:
        queue.dma_start(
            out=plane[32 * q : 32 * q + 4, :, :].bitcast(I32),
            in_=scales[:, 4 * q : 4 * q + 4, :].rearrange("m r w -> r m w").bitcast(I32),
        )


def tile_moe_shf_glu_gelu_kernel(
    tc, x_words, x_scales, w1_words, w1_scales, w3_words, w3_scales, w2_words, w2_scales,
    w1s_words, w1s_scales, w3s_words, w3s_scales, w2s_words, w2s_scales, gate, offs, pos1, pos2, out,
):
    nc = tc.nc
    with ExitStack() as ctx:
        keep = ctx.enter_context(tc.tile_pool(name="keep", bufs=1))
        psum = ctx.enter_context(tc.psum_pool(name="psum", bufs=1))

        def tiles(name, count, shape, dtype):
            return [keep.tile(shape, dtype, name="%s%d" % (name, k), align_bytes=64) for k in range(count)]

        offs_t = keep.tile([P, S // 16], U16, name="offs_t")
        pos1_t = keep.tile([P, T // 16], U16, name="pos1_t")
        pos2_t = keep.tile([P, T // 16], U16, name="pos2_t")
        xw = keep.tile([P, T], I32, name="xw", align_bytes=64)
        xs = keep.tile([P, 1, T], U8, name="xs", align_bytes=64)
        s1 = keep.tile([P, E, H], U8, name="s1", align_bytes=64)
        s3 = keep.tile([P, E, H], U8, name="s3", align_bytes=64)
        s2 = keep.tile([P, E, N], U8, name="s2", align_bytes=64)
        s1s = keep.tile([P, 1, H], U8, name="s1s", align_bytes=64)
        s3s = keep.tile([P, 1, H], U8, name="s3s", align_bytes=64)
        s2s = keep.tile([P, 1, N], U8, name="s2s", align_bytes=64)
        w1s = keep.tile([P, H], I32, name="w1s", align_bytes=64)
        w3s = keep.tile([P, H], I32, name="w3s", align_bytes=64)
        w2s = keep.tile([P, N], I32, name="w2s", align_bytes=64)
        gate_t = keep.tile([P, 2, T], F32, name="gate_t")
        ident = keep.tile([P, P], F32, name="ident")

        nc.gpsimd.memset(s2[:].bitcast(I32), 0)
        for plane in (xs, s1s, s1, ident, s3, s3s, s2s):
            nc.vector.memset(plane[:].bitcast(I32), 0)
        make_identity(nc, ident[:], nomemset=True)

        w1, w3, w2 = {}, {}, {}

        def load_fp4(queue, words, held, name, lo, hi):
            t = keep.tile([P, hi - lo, words.shape[3]], U8, name="%s_%d" % (name, lo), align_bytes=64)
            queue.dma_start(out=t[:].bitcast(I32), in_=words[lo:hi, 0].rearrange("e p n -> p e n").bitcast(I32))
            for e in range(lo, hi):
                held[e] = t[:, e - lo, :]

        def load_fp8(queue, t, words):
            queue.dma_start(out=t[:], in_=words[0].rearrange("p n d -> p (n d)").bitcast(I32))

        def load_gate(c):
            third = slice(c * G, (c + 1) * G)
            nc.sync.dma_start(out=gate_t[:, :, third], in_=gate.rearrange("r p t -> p r t")[:, :, third])

        ports = (0, 2, 1, 3)
        nc.sync.dma_start(offs_t[:], offs)
        load_scales(nc.sync, (0, 2), xs[:], x_scales)
        load_scales(nc.scalar, (1, 3), xs[:], x_scales)
        load_fp8(nc.sync, xw, x_words)
        load_fp8(nc.sync, w1s, w1s_words)
        load_scales(nc.scalar, (0,), s1s[:], w1s_scales)
        load_scales(nc.sync, (2, 1, 3), s1s[:], w1s_scales)
        load_scales(nc.sync, ports, s1[:], w1_scales[:, 0])
        load_scales(nc.sync, ports, s3[:], w3_scales[:, 0])
        load_fp4(nc.sync, w1_words, w1, "w1", 0, 2)
        load_fp4(nc.sync, w3_words, w3, "w3", 0, 2)
        load_fp4(nc.sync, w1_words, w1, "w1", 2, 4)
        load_fp4(nc.sync, w1_words, w1, "w1", 4, 6)
        load_fp4(nc.sync, w3_words, w3, "w3", 2, 4)
        load_fp4(nc.sync, w3_words, w3, "w3", 4, 6)
        load_fp8(nc.sync, w3s, w3s_words)
        load_scales(nc.sync, ports, s3s[:], w3s_scales)
        load_fp4(nc.sync, w2_words, w2, "w2", 0, 6)
        load_scales(nc.sync, ports, s2[:], w2_scales[:, 0])
        load_fp8(nc.sync, w2s, w2s_words)
        nc.sync.dma_start(pos1_t[:], pos1)
        nc.sync.dma_start(pos2_t[:], pos2)
        load_gate(0)
        load_scales(nc.sync, ports, s2s[:], w2s_scales)
        load_gate(1)
        load_gate(2)

        y = [keep.tile([P, S], F32, name="y%d" % v) for v in range(2)]
        banks = [psum.tile([P, H], F32, name="bank%d" % k) for k in range(8)]
        scalar_ring, vector_ring = banks[0:4], banks[4:8]
        got_words, got_scales, gate_sums, shared, units = {}, {}, {}, {}, {}
        acts = tiles("act", 2 * GROUPS, [P, 2, P, 2], F32)
        turned = tiles("ht", GROUPS, [P, 4 * G], BF16)
        hidden = [t[:] for t in tiles("h", 2 * GROUPS - 3, [P, H], BF16)]
        spent = acts[len(hidden)][:].rearrange("p u m e -> p (u m e)").bitcast(BF16)
        hidden = hidden + [turned[E - 1][:, 0:H], turned[E - 1][:, H : 2 * H], spent[:, 0:H]]
        codes = tiles("hq", GROUPS, [P, G], U32)
        code_scales = tiles("hs", GROUPS, [P, G], U8)

        def take(ring):
            ring[:] = ring[1:] + ring[:1]
            return ring[-1]

        def gather(held, window, name, e, count):
            into = keep.tile([P, count * C], window.dtype, name="%s%d" % (name, e), align_bytes=64)
            nc.vector.tensor_copy(into[:], window.indirect(offs_t[:, e * C // 16 : (e + count) * C // 16]))
            for i in range(count):
                held[e + i] = into[:, i * C : (i + 1) * C]

        def first_product(bank, k, routed, routed_scales, common, common_scales):
            g, j = divmod(k, 2)
            if g < E:
                cols = slice(j * P, (j + 1) * P)
                words, scales = got_words[g][:, cols], got_scales[g][:, cols]
                w, ws = routed[g].bitcast(FP4X4), routed_scales[:, g, :]
            else:
                cols = slice((k - 2 * E) * P, (k - 2 * E + 1) * P)
                words, scales = xw[:, cols], xs[:, 0, cols]
                w, ws = common[:].bitcast(FP8X4), common_scales[:, 0, :]
            nc.tensor.matmul_mx(
                out=bank[:], lhsT=words.bitcast(FP8X4), lhsT_scale=scales, rhs=w, rhs_scale=ws, start=True, stop=True
            )
            return bank[:].rearrange("p (m u e) -> p u m e", u=2, e=2)

        def gelu_side(k, ring=scalar_ring):
            sums = first_product(take(ring), k, w1, s1, w1s, s1s)
            nc.scalar.activation(acts[k][:], sums, GELU)

        def gate_side(k):
            gate_sums[k] = first_product(take(vector_ring), k, w3, s3, w3s, s3s)

        def multiply(k):
            into = hidden[k].rearrange("p (u m e) -> p u m e", u=2, e=2)
            nc.vector.tensor_tensor(into, gate_sums[k], acts[k][:], MULT)

        def multiply_and_refill(k):
            multiply(k)
            gate_side(k + len(vector_ring))

        def turn(g, bank):
            tr = bank[:].rearrange("p (j u r) -> p j u r", j=2, u=2)
            for j in (1, 0):
                pairs = hidden[2 * g + j].bitcast(F32)
                for u in range(2):
                    nc.tensor.transpose(tr[:, j, u, :], pairs[:, u * P : (u + 1) * P], ident[:])
            nc.scalar.copy(
                turned[g][:].bitcast(F32).rearrange("p (j r u) -> p j r u", j=2, u=2), tr.rearrange("p j u r -> p j r u")
            )

        def quantise(g):
            nc.vector.quantize_mx(out=codes[g][:].bitcast(FP8X4), scales=code_scales[g][:], in_=turned[g][:])

        def by_feature(acc, g, cols, w, ws):
            nc.tensor.matmul_mx(
                out=acc, lhsT=w, lhsT_scale=ws, rhs=codes[g][:, cols].bitcast(FP8X4), rhs_scale=code_scales[g][:, cols],
                start=True, stop=True,
            )

        def second_routed(v, experts, bank):
            low = min(experts)
            for g in experts:
                w = w2[g][:, 2 * v * P : 2 * (v + 1) * P].bitcast(FP4X4)
                by_feature(bank[:, (g - low) * G : (g - low + 1) * G], g, slice(0, G), w, s2[:, g, v * P : (v + 1) * P])
            nc.scalar.copy(y[v][:, low * C : (low + 2) * C], bank[:])

        def second_shared(c, bank):
            widths = [N if b < UPPER_BLOCKS else P for b in (2 * c, 2 * c + 1)]
            held = keep.tile([P, sum(widths)], F32, name="shared%d" % c)
            for j, width in enumerate(widths):
                cols = slice(j * widths[0], j * widths[0] + width)
                nc.tensor.matmul_mx(
                    out=bank[:, cols], lhsT=codes[E + c][:, j * P : (j + 1) * P].bitcast(FP8X4),
                    lhsT_scale=code_scales[E + c][:, j * P : (j + 1) * P],
                    rhs=w2s[:, 0:width].bitcast(FP8X4), rhs_scale=s2s[:, 0, 0:width], start=True, stop=True,
                )
                shared[2 * c + j] = held[:, cols]
            nc.scalar.copy(held[:], bank[:, 0 : sum(widths)])

        def picks(name, v, tokens):
            first, second, part, res = tiles(name, 4, [P, tokens.stop - tokens.start], F32)
            for r, (into, places) in enumerate(((first, pos1_t), (second, pos2_t))):
                window = y[v][:].indirect(places[:, tokens.start // 16 : tokens.stop // 16])
                nc.vector.tensor_tensor(into[:], window, gate_t[:, r, tokens], MULT)
            return first, second, part, res

        def turn_and_add(into, terms):
            for k, term in enumerate(terms):
                nc.tensor.matmul(into, term, ident[:], start=(k == 0), stop=(k == len(terms) - 1), is_transpose=True)

        def keep_clock_up(bank):
            for k in range(2):
                first_product(bank, 2 * E + k, w1, s1, w1s, s1s)

        def there(v, tokens, bank):
            first, second, part, res = units[v, tokens.start]
            width = tokens.stop - tokens.start
            for col in range(0, width, P):
                turn_and_add(bank[:, col : col + P], (second[:, col : col + P], first[:, col : col + P]))
            nc.scalar.copy(part[:], bank[:, 0:width])

        def back(v, tokens, bank):
            first, second, part, res = units[v, tokens.start]
            width = tokens.stop - tokens.start
            for col in range(0, width, P):
                ys = shared[(tokens.start + col) // P][:, v * P : (v + 1) * P]
                turn_and_add(bank[:, col : col + P], (part[:, col : col + P], ys))
            nc.scalar.copy(res[:], bank[:, 0:width])
            nc.scalar.dma_start(out=out[v * P : (v + 1) * P, tokens], in_=res[:])

        for e in range(0, E, 2):
            gather(got_scales, xs[:, 0, :], "got_scales", e, 2)
        for e in range(0, E, 2):
            gather(got_words, xw[:].bitcast(U32), "got_words", e, 2)

        for i, k in enumerate(list(range(2 * E, 2 * GROUPS)) + [0, 1]):
            gelu_side(k, scalar_ring if i < len(scalar_ring) else vector_ring)
        for k in range(2 * E - 1):
            if k >= len(vector_ring):
                multiply(k - len(vector_ring))
            if k > 0:
                gelu_side(k + 1)
            gate_side(k)
        multiply_and_refill(7)
        turn(0, take(scalar_ring))
        turn(1, take(scalar_ring))
        for k in (8, 9, 10):
            multiply_and_refill(k)
        turn(2, take(scalar_ring))
        turn(3, take(scalar_ring))
        multiply_and_refill(11)
        quantise(0)
        quantise(1)
        multiply_and_refill(12)
        turn(4, take(scalar_ring))
        turn(5, take(scalar_ring))
        quantise(2)
        quantise(3)
        multiply_and_refill(13)
        quantise(4)
        quantise(5)
        for g in range(0, E, 2):
            second_routed(0, (g + 1, g), take(scalar_ring))
        for k in (14, 15, 16, 17):
            multiply(k)
        for g in range(E, GROUPS):
            turn(g, take(scalar_ring))

        by_vector = slice(UPPER_BLOCKS * P, T)
        stretches = [(0, slice(c * G, (c + 1) * G)) for c in range(T // G)]
        stretches = stretches + [(1, slice(0, G))] + [(1, slice(t, t + P)) for t in range(G, by_vector.start, P)]
        for i, (v, tokens) in enumerate(stretches):
            units[v, tokens.start] = picks("unit%d_" % i, v, tokens)
            if v == 0:
                quantise(E + i)
                second_shared(i, take(scalar_ring))
            if i == T // G - 1:
                upper = take(vector_ring)
                pieces = []
                for t in range(by_vector.start, T, P):
                    if t % G == 0 or t == by_vector.start:
                        stop = (t // G + 1) * G
                        cols = slice(t - by_vector.start, stop - by_vector.start)
                        by_feature(upper[:, cols], E + t // G, slice(t % G, G), w2s[:, P:N].bitcast(FP8X4), s2s[:, 0, P:N])
                        pieces.append((cols, slice(t, stop)))
            bank = take(scalar_ring)
            if i < 4:
                keep_clock_up(bank)
            there(v, tokens, bank)
            if i == 0:
                for e in range(0, E, 2):
                    second_routed(1, (e, e + 1), take(vector_ring))
            else:
                back(*stretches[i - 1], take(scalar_ring))
        back(*stretches[-1], take(scalar_ring))

        first, second, part, res = picks("late", 1, by_vector)
        for cols, tokens in reversed(pieces):
            nc.vector.tensor_tensor(part[:, cols], upper[:, cols], first[:, cols], ADD)
        for cols, tokens in reversed(pieces):
            nc.vector.tensor_tensor(res[:, cols], part[:, cols], second[:, cols], ADD)
            nc.sync.dma_start(out=out[P:N, tokens], in_=res[:, cols])
